import numpy as np
import ml_dtypes


def mxq(x, axis, fmt="e4m3"):
    dtype, down = {"e4m3": (ml_dtypes.float8_e4m3fn, 7), "e5m2": (ml_dtypes.float8_e5m2, 14)}[fmt]
    v = np.moveaxis(np.asarray(x, np.float32).astype(ml_dtypes.bfloat16).astype(np.float64), axis, -1)
    blocks = v.reshape(v.shape[:-1] + (-1, 32))
    amax = np.abs(blocks).max(-1, keepdims=True)
    byte = np.maximum(np.where(amax > 0, np.frexp(amax)[1] - 1 + 127, 0) - down, 1)
    scale = np.exp2(byte - 127.0)
    codes = (blocks / scale).astype(np.float32).astype(dtype).astype(np.float64)
    return np.moveaxis((codes * scale).reshape(v.shape), -1, axis)


WIDE = False


def mx_kscale(k):
    if not WIDE:
        return np.ones(k)
    levels = np.array([10, -10, 5, -5, 0])
    if k % 512:
        return np.exp2(np.random.permutation(np.resize(levels, k // 32))).repeat(32)
    a = np.empty((k // 512, 16))
    for p in range(k // 512):
        a[p, :8] = np.random.permutation(np.resize(levels, 8))
        for g in range(8):
            far = levels[np.abs(levels - a[p, g]) >= 10]
            a[p, g + 8] = far[np.random.randint(len(far))]
    return np.exp2(a.ravel()).repeat(32)


def f64(x):
    return np.asarray(x).astype(np.float64)


def striped(idx):
    return np.tile(idx.reshape(-1, 16).T, (8, 1)).astype(np.uint16)


def unstriped(offs):
    return offs[:16].T.reshape(-1).astype(np.int64)


def pack_weight(w):
    k, n = w.shape
    w = f64(np.asarray(w, np.float32).astype(ml_dtypes.bfloat16)).reshape(k // 32, 32, n)
    amax = np.abs(w).max(1)
    byte = np.clip(np.where(amax > 0, np.frexp(amax)[1] - 1 + 127 - 7, 1), 1, 254)
    scaled = (w * np.exp2(127.0 - byte)[:, None, :]).reshape(k, n).astype(np.float32)
    words = np.ascontiguousarray(scaled.reshape(k // 512, 128, 4, n).transpose(0, 1, 3, 2)).astype(ml_dtypes.float8_e4m3fn).view(np.uint8)
    return words, np.ascontiguousarray(byte.astype(np.uint8).reshape(k // 512, 16, n))


def unpack_weight(words, scales):
    g, p, n, _ = words.shape
    vals = np.ascontiguousarray(words).view(ml_dtypes.float8_e4m3fn).astype(np.float64) * np.repeat(np.exp2(scales.astype(np.float64) - 127.0), 8, axis=1)[..., None]
    return vals.transpose(0, 1, 3, 2).reshape(g * 512, n)


def planes(y):
    n, m = y.shape
    v = y.astype(np.float32).astype(ml_dtypes.bfloat16).astype(np.float64).reshape(n // 32, 32, m)
    top = np.abs(v).max(1)
    byte = np.clip(np.where(top > 0, np.frexp(top)[1] - 1 + 127 - 7, 1), 1, 254)
    codes = (v * np.exp2(127.0 - byte)[:, None, :]).reshape(n, m).astype(np.float32).astype(ml_dtypes.float8_e4m3fn).view(np.uint8)
    words = codes.reshape(n // 512, 128, 4, m).transpose(0, 1, 3, 2)
    return np.ascontiguousarray(words), np.ascontiguousarray(byte.astype(np.uint8).reshape(n // 512, 16, m))


def silu(v):
    return v / (1.0 + np.exp(-np.maximum(v, -700.0)))


K, T, S, W, H, N = 512, 2048, 512, 1024, 512, 512


def setup_inputs():
    n = np.random.standard_normal
    s = mx_kscale(K)[:, None]
    u = mx_kscale(H)
    packed_xT = pack_weight(n((K, T)) * s)
    packed_eT = pack_weight(n((K, W)) * s)
    packed_yT = pack_weight(n((K, W)) * s)
    packed_w4 = pack_weight(n((H, N)) / np.sqrt(H) / u[:, None])
    return {
        "x_words": packed_xT[0],
        "x_scales": packed_xT[1],
        "e_words": packed_eT[0],
        "e_scales": packed_eT[1],
        "y_words": packed_yT[0],
        "y_scales": packed_yT[1],
        "w1": (n((K, H)) / np.sqrt(3 * K) / s * u).astype(np.float32),
        "w2": (n((K, H)) / np.sqrt(3 * K) / s * u).astype(np.float32),
        "w3": (n((K, H)) / np.sqrt(3 * K) / s * u).astype(np.float32),
        "w4_words": packed_w4[0],
        "w4_scales": packed_w4[1],
        "offs": striped(np.random.permutation(T)[:S]),
        "tok": striped(np.random.permutation(W)[:S]),
        "row": striped(np.random.permutation(W)[:S]),
    }


def reference(x_words, x_scales, e_words, e_scales, y_words, y_scales, w1, w2, w3, w4_words, w4_scales, offs, tok, row):
    xq = unpack_weight(x_words, x_scales)[:, unstriped(offs)]
    e_tok = unpack_weight(e_words, e_scales)[:, unstriped(tok)]
    y_row = unpack_weight(y_words, y_scales)[:, unstriped(row)]
    h = silu(mxq(f64(w1), 0, "e4m3").T @ xq + mxq(f64(w2), 0, "e4m3").T @ e_tok + mxq(f64(w3), 0, "e4m3").T @ y_row)
    out_0 = unpack_weight(w4_words, w4_scales).T @ mxq(h, 0, "e4m3")
    return (out_0,) + planes(out_0)

@@ -1,0 +1,200 @@
+from contextlib import ExitStack
+
+import concourse.mybir as mybir
+
+K, T, S, W, H, N = 512, 2048, 512, 1024, 512, 512
+FLOPS = 2 * (3 * K * H * S + H * N * S)
+
+F32 = mybir.dt.float32
+BF16 = mybir.dt.bfloat16
+I32 = mybir.dt.int32
+U32 = mybir.dt.uint32
+U16 = mybir.dt.uint16
+U8 = mybir.dt.uint8
+FP8X4 = mybir.dt.float8_e4m3fn_x4
+SILU = mybir.ActivationFunctionType.Silu
+
+P = 128
+PACK = 4
+CHUNK = 128
+CHUNKS = S // CHUNK
+LIST_COLS = S // 16
+
+
+def tile_picked_zlayout_silu_po_kernel(
+    tc, x_words, x_scales, e_words, e_scales, y_words, y_scales, w1, w2, w3, w4_words, w4_scales, offs, tok, row,
+    out_0, out_1, out_2,
+):
+    nc = tc.nc
+    with ExitStack() as ctx:
+        keep = ctx.enter_context(tc.tile_pool(name="keep", bufs=1))
+        psum = ctx.enter_context(tc.psum_pool(name="psum", bufs=1))
+
+        def words_view(words):
+            return words[0].rearrange("p n t -> p (n t)").bitcast(I32)
+
+        tables = {"e": (e_words, e_scales, tok, W, 4), "x": (x_words, x_scales, offs, T, 0), "y": (y_words, y_scales, row, W, 8)}
+        W4_ROW = 12
+
+        plane = {}
+        for name in ("x", "e", "y"):
+            plane[name] = keep.tile([P, tables[name][3]], U8, name="plane_" + name, align_bytes=64)
+        w4_plane = keep.tile([P, N], U8, name="w4_plane", align_bytes=64)
+        nc.vector.memset(plane["e"][:, : W // 2].bitcast(I32), 0)
+        nc.gpsimd.memset(plane["e"][:, W // 2 :].bitcast(I32), 0)
+        nc.vector.memset(plane["y"][:].bitcast(I32), 0)
+        nc.gpsimd.memset(w4_plane[:].bitcast(I32), 0)
+        nc.vector.memset(plane["x"][:].bitcast(I32), 0)
+
+        def load_scales(tile, scales, first, quadrants):
+            for q in quadrants:
+                nc.sync.dma_start(out=tile[32 * q + first : 32 * q + first + 4, :].bitcast(I32), in_=scales[0, 4 * q : 4 * q + 4, :].bitcast(I32))
+
+        raw, lists, table = {}, {}, {}
+
+        def load_w(name, w):
+            raw[name] = keep.tile([P, PACK, H], F32, name="raw_" + name)
+            nc.sync.dma_start(out=raw[name][:], in_=w.rearrange("(p j) c -> p j c", j=PACK))
+
+        def load_list(name):
+            lists[name] = keep.tile([P, LIST_COLS], U16, name="list_" + name)
+            nc.sync.dma_start(lists[name][:], tables[name][2])
+
+        def load_table(name):
+            table[name] = keep.tile([P, tables[name][3]], I32, name="table_" + name, tag="table_" + name, align_bytes=64)
+            nc.sync.dma_start(out=table[name][:], in_=words_view(tables[name][0]))
+
+        load_list("e")
+        load_table("e")
+        load_list("x")
+        load_list("y")
+        load_scales(plane["e"], e_scales, tables["e"][4], range(0, 3))
+        load_w("x", w1)
+        load_scales(plane["e"], e_scales, tables["e"][4], range(3, 4))
+        load_scales(plane["y"], y_scales, tables["y"][4], range(4))
+        load_w("e", w2)
+        load_scales(plane["x"], x_scales, tables["x"][4], range(4))
+        load_w("y", w3)
+        load_scales(w4_plane, w4_scales, W4_ROW, range(4))
+        load_table("x")
+        load_table("y")
+        w4_raw = keep.tile([P, N], I32, name="w4_raw", align_bytes=64)
+        nc.sync.dma_start(out=w4_raw[:], in_=words_view(w4_words))
+
+        picked_scales, picked = {}, {}
+
+        def gather_scales(name):
+            picked_scales[name] = keep.tile([P, S], U8, name="picked_scales_" + name, align_bytes=64)
+            nc.vector.tensor_copy(picked_scales[name][:], plane[name][:].indirect(lists[name][:]))
+
+        def gather_words(name, c0, c1):
+            piece = keep.tile([P, c1 - c0], U32, name="picked_%s_%d" % (name, c0), align_bytes=64)
+            nc.vector.tensor_copy(piece[:], table[name][:].bitcast(U32).indirect(lists[name][:, c0 // 16 : c1 // 16]))
+            for c in range(c0 // CHUNK, c1 // CHUNK):
+                picked[name, c] = piece[:, c * CHUNK - c0 : (c + 1) * CHUNK - c0]
+
+        grouped, w_codes, w_scales = {}, {}, {}
+
+        def round_w(name, copy, t0, t1):
+            grouped[name, t0] = keep.tile([P, t1 - t0, P, PACK], BF16, name="grouped_%s_%d" % (name, t0), align_bytes=64)
+            copy(
+                grouped[name, t0][:].rearrange("p t m j -> p m j t"),
+                raw[name][:].rearrange("p j (m t) -> p m j t", t=PACK)[:, :, :, t0:t1],
+            )
+
+        def quantize_w(name, t0, t1):
+            codes = keep.tile([P, (t1 - t0) * P], U32, name="w_codes_%s_%d" % (name, t0), align_bytes=64)
+            scales = keep.tile([P, (t1 - t0) * P], U8, name="w_scales_%s_%d" % (name, t0), align_bytes=64)
+            nc.vector.quantize_mx(out=codes[:].bitcast(FP8X4), scales=scales[:], in_=grouped[name, t0][:].rearrange("p t m j -> p (t m j)"))
+            for t in range(t0, t1):
+                w_codes[name, t] = codes[:, (t - t0) * P : (t - t0 + 1) * P]
+                w_scales[name, t] = scales[:, (t - t0) * P : (t - t0 + 1) * P]
+
+        gather_words("e", 0, S)
+        gather_scales("e")
+        gather_scales("y")
+        round_w("x", nc.scalar.copy, 0, PACK)
+        gather_scales("x")
+        quantize_w("x", 0, PACK)
+        round_w("e", nc.scalar.copy, 0, PACK)
+        quantize_w("e", 0, PACK)
+        round_w("y", nc.scalar.copy, 0, 2)
+        round_w("y", nc.vector.tensor_copy, 2, PACK)
+        quantize_w("y", 0, 2)
+        quantize_w("y", 2, PACK)
+        gather_words("x", 0, S)
+        h_banks = [psum.tile([P, PACK, CHUNK], F32, name="h_bank_%d" % c) for c in range(CHUNKS)]
+
+        def first_pass(c, t, name):
+            nc.tensor.matmul_mx(
+                out=h_banks[c][:, t, :],
+                lhsT=w_codes[name, t].bitcast(FP8X4),
+                lhsT_scale=w_scales[name, t],
+                rhs=picked[name, c].bitcast(FP8X4),
+                rhs_scale=picked_scales[name][tables[name][4] :, c * CHUNK : (c + 1) * CHUNK],
+                start=(name == "e"),
+                stop=(name == "y"),
+            )
+
+        for name in ("e", "x"):
+            for c in range(CHUNKS):
+                first_pass(c, 0, name)
+        for c in range(CHUNKS):
+            gather_words("y", c * CHUNK, (c + 1) * CHUNK)
+        w4_dealt_scales = keep.tile([P, N], U8, name="w4_dealt_scales", tag="table_x", align_bytes=64)
+        nc.vector.tensor_copy(w4_dealt_scales[:].rearrange("p (t m) -> p m t", t=PACK), w4_plane[:].rearrange("p (m t) -> p m t", t=PACK))
+        w4_dealt = keep.tile([P, N], I32, name="w4_dealt", tag="table_y", align_bytes=64)
+        nc.vector.tensor_copy(w4_dealt[:].rearrange("p (t m) -> p m t", t=PACK), w4_raw[:].rearrange("p (m t) -> p m t", t=PACK))
+
+        out_words = keep.tile([P, S], I32, name="out_words", align_bytes=64)
+        out_scales = keep.tile([P, S], U8, name="out_scales", align_bytes=64)
+        out_rows = out_0.rearrange("(p t) j -> p t j", t=PACK)
+        hidden, result = {}, {}
+
+        def first_product(c):
+            bank = h_banks[c]
+            first_pass(c, 0, "y")
+            for t in range(1, PACK):
+                for name in ("e", "x", "y"):
+                    first_pass(c, t, name)
+            h_bf16 = keep.tile([P, CHUNK, PACK], BF16, name="h_bf16_%d" % c, align_bytes=64)
+            nc.scalar.activation(h_bf16[:], bank[:].rearrange("p t n -> p n t"), SILU)
+            h_codes = keep.tile([P, CHUNK], U32, name="h_codes_%d" % c, align_bytes=64)
+            h_scales = keep.tile([P, CHUNK], U8, name="h_scales_%d" % c, align_bytes=64)
+            nc.vector.quantize_mx(out=h_codes[:].bitcast(FP8X4), scales=h_scales[:], in_=h_bf16[:].rearrange("p n t -> p (n t)"))
+            hidden[c] = (h_codes, h_scales)
+
+        def second_product(c):
+            cols = slice(c * CHUNK, (c + 1) * CHUNK)
+            h_codes, h_scales = hidden[c]
+            bank = psum.tile([P, PACK, CHUNK], F32, name="out_bank_%d" % c)
+            for t in range(PACK):
+                m_cols = slice(t * P, (t + 1) * P)
+                nc.tensor.matmul_mx(
+                    out=bank[:, t, :],
+                    lhsT=w4_dealt[:, m_cols].bitcast(FP8X4),
+                    lhsT_scale=w4_dealt_scales[W4_ROW:, m_cols],
+                    rhs=h_codes[:].bitcast(FP8X4),
+                    rhs_scale=h_scales[:],
+                    start=True,
+                    stop=True,
+                )
+            result[c] = keep.tile([P, PACK, CHUNK], F32, name="result_%d" % c, align_bytes=64)
+            nc.scalar.copy(result[c][:], bank[:])
+            nc.sync.dma_start(out=out_rows[:, :, cols], in_=result[c][:])
+            out_bf16 = keep.tile([P, CHUNK, PACK], BF16, name="out_bf16_%d" % c, align_bytes=64)
+            nc.vector.tensor_copy(out_bf16[:], result[c][:].rearrange("p t n -> p n t"))
+            nc.vector.quantize_mx(out=out_words[:, cols].bitcast(FP8X4), scales=out_scales[:, cols], in_=out_bf16[:].rearrange("p n t -> p (n t)"))
+            if c % 2 == 1:
+                half = slice((c - 1) * CHUNK, (c + 1) * CHUNK)
+                nc.sync.dma_start(out=words_view(out_1)[:, half], in_=out_words[:, half])
+
+        for c in range(CHUNKS + 2):
+            if c < CHUNKS:
+                first_product(c)
+            if c >= 2:
+                second_product(c - 2)
+
+        for q in range(4):
+            queue = nc.sync if q % 2 == 0 else nc.scalar
+            queue.dma_start(out=out_2[0, 4 * q : 4 * q + 4, :].bitcast(I32), in_=out_scales[32 * q : 32 * q + 4, :].bitcast(I32))

@@ -19,6 +19,9 @@ PACK = 4
 CHUNK = 128
 CHUNKS = S // CHUNK
 LIST_COLS = S // 16
+WARM = 4
+TABLE_AT = {"x": 0, "y": 4 * T, "e": 4 * (T + W)}
+PLANE_X_AT = 4 * (T + 2 * W)
 
 
 def tile_picked_zlayout_silu_po_kernel(
@@ -28,6 +31,7 @@ def tile_picked_zlayout_silu_po_kernel(
     nc = tc.nc
     with ExitStack() as ctx:
         keep = ctx.enter_context(tc.tile_pool(name="keep", bufs=1))
+        reused = ctx.enter_context(tc.tile_pool(name="reused", bufs=1))
         psum = ctx.enter_context(tc.psum_pool(name="psum", bufs=1))
 
         def words_view(words):
@@ -37,7 +41,8 @@ def tile_picked_zlayout_silu_po_kernel(
         W4_ROW = 12
 
         plane = {}
-        for name in ("x", "e", "y"):
+        plane["x"] = reused.tile([P, T], U8, name="plane_x", align_bytes=64, offset=PLANE_X_AT)
+        for name in ("e", "y"):
             plane[name] = keep.tile([P, tables[name][3]], U8, name="plane_" + name, align_bytes=64)
         w4_plane = keep.tile([P, N], U8, name="w4_plane", align_bytes=64)
         nc.vector.memset(plane["e"][:, : W // 2].bitcast(I32), 0)
@@ -61,7 +66,7 @@ def tile_picked_zlayout_silu_po_kernel(
             nc.sync.dma_start(lists[name][:], tables[name][2])
 
         def load_table(name):
-            table[name] = keep.tile([P, tables[name][3]], I32, name="table_" + name, tag="table_" + name, align_bytes=64)
+            table[name] = reused.tile([P, tables[name][3]], I32, name="table_" + name, align_bytes=64, offset=TABLE_AT[name])
             nc.sync.dma_start(out=table[name][:], in_=words_view(tables[name][0]))
 
         load_list("e")
@@ -88,15 +93,22 @@ def tile_picked_zlayout_silu_po_kernel(
             nc.vector.tensor_copy(picked_scales[name][:], plane[name][:].indirect(lists[name][:]))
 
         def gather_words(name, c0, c1):
-            piece = keep.tile([P, c1 - c0], U32, name="picked_%s_%d" % (name, c0), align_bytes=64)
+            if name == "y":
+                piece = reused.tile([P, c1 - c0], U32, name="picked_%s_%d" % (name, c0), align_bytes=64, offset=TABLE_AT["x"] + 4 * c0)
+            else:
+                piece = keep.tile([P, c1 - c0], U32, name="picked_%s_%d" % (name, c0), align_bytes=64)
             nc.vector.tensor_copy(piece[:], table[name][:].bitcast(U32).indirect(lists[name][:, c0 // 16 : c1 // 16]))
             for c in range(c0 // CHUNK, c1 // CHUNK):
                 picked[name, c] = piece[:, c * CHUNK - c0 : (c + 1) * CHUNK - c0]
+            return piece
 
         grouped, w_codes, w_scales = {}, {}, {}
 
         def round_w(name, copy, t0, t1):
-            grouped[name, t0] = keep.tile([P, t1 - t0, P, PACK], BF16, name="grouped_%s_%d" % (name, t0), align_bytes=64)
+            if (name, t0) == ("y", 2):
+                grouped[name, t0] = reused.tile([P, t1 - t0, P, PACK], BF16, name="grouped_%s_%d" % (name, t0), align_bytes=64, offset=PLANE_X_AT + H)
+            else:
+                grouped[name, t0] = keep.tile([P, t1 - t0, P, PACK], BF16, name="grouped_%s_%d" % (name, t0), align_bytes=64)
             copy(
                 grouped[name, t0][:].rearrange("p t m j -> p m j t"),
                 raw[name][:].rearrange("p j (m t) -> p m j t", t=PACK)[:, :, :, t0:t1],
@@ -104,13 +116,16 @@ def tile_picked_zlayout_silu_po_kernel(
 
         def quantize_w(name, t0, t1):
             codes = keep.tile([P, (t1 - t0) * P], U32, name="w_codes_%s_%d" % (name, t0), align_bytes=64)
-            scales = keep.tile([P, (t1 - t0) * P], U8, name="w_scales_%s_%d" % (name, t0), align_bytes=64)
+            if name == "e":
+                scales = reused.tile([P, (t1 - t0) * P], U8, name="w_scales_%s_%d" % (name, t0), align_bytes=64, offset=PLANE_X_AT)
+            else:
+                scales = keep.tile([P, (t1 - t0) * P], U8, name="w_scales_%s_%d" % (name, t0), align_bytes=64)
             nc.vector.quantize_mx(out=codes[:].bitcast(FP8X4), scales=scales[:], in_=grouped[name, t0][:].rearrange("p t m j -> p (t m j)"))
             for t in range(t0, t1):
                 w_codes[name, t] = codes[:, (t - t0) * P : (t - t0 + 1) * P]
                 w_scales[name, t] = scales[:, (t - t0) * P : (t - t0 + 1) * P]
 
-        gather_words("e", 0, S)
+        picked_e = gather_words("e", 0, S)
         gather_scales("e")
         gather_scales("y")
         round_w("x", nc.scalar.copy, 0, PACK)
@@ -122,7 +137,8 @@ def tile_picked_zlayout_silu_po_kernel(
         round_w("y", nc.vector.tensor_copy, 2, PACK)
         quantize_w("y", 0, 2)
         quantize_w("y", 2, PACK)
-        gather_words("x", 0, S)
+        gather_words("x", 0, S // 2)
+        gather_words("x", S // 2, S)
         h_banks = [psum.tile([P, PACK, CHUNK], F32, name="h_bank_%d" % c) for c in range(CHUNKS)]
 
         def first_pass(c, t, name):
@@ -136,14 +152,26 @@ def tile_picked_zlayout_silu_po_kernel(
                 stop=(name == "y"),
             )
 
-        for name in ("e", "x"):
-            for c in range(CHUNKS):
-                first_pass(c, 0, name)
+        for c in range(CHUNKS):
+            first_pass(c, 0, "e")
+        for t in range(WARM):
+            warm = psum.tile([P, S], F32, name="warm", tag="out_bank_%d" % t)
+            nc.tensor.matmul_mx(
+                out=warm[:],
+                lhsT=w_codes["e", t].bitcast(FP8X4),
+                lhsT_scale=w_scales["e", t],
+                rhs=picked_e[:].bitcast(FP8X4),
+                rhs_scale=picked_scales["e"][tables["e"][4] :, :],
+                start=True,
+                stop=True,
+            )
+        for c in range(CHUNKS):
+            first_pass(c, 0, "x")
         for c in range(CHUNKS):
             gather_words("y", c * CHUNK, (c + 1) * CHUNK)
-        w4_dealt_scales = keep.tile([P, N], U8, name="w4_dealt_scales", tag="table_x", align_bytes=64)
+        w4_dealt_scales = reused.tile([P, N], U8, name="w4_dealt_scales", align_bytes=64, offset=TABLE_AT["y"] + 4 * N)
         nc.vector.tensor_copy(w4_dealt_scales[:].rearrange("p (t m) -> p m t", t=PACK), w4_plane[:].rearrange("p (m t) -> p m t", t=PACK))
-        w4_dealt = keep.tile([P, N], I32, name="w4_dealt", tag="table_y", align_bytes=64)
+        w4_dealt = reused.tile([P, N], I32, name="w4_dealt", align_bytes=64, offset=TABLE_AT["y"])
         nc.vector.tensor_copy(w4_dealt[:].rearrange("p (t m) -> p m t", t=PACK), w4_raw[:].rearrange("p (m t) -> p m t", t=PACK))
 
         out_words = keep.tile([P, S], I32, name="out_words", align_bytes=64)
@@ -167,7 +195,7 @@ def tile_picked_zlayout_silu_po_kernel(
         def second_product(c):
             cols = slice(c * CHUNK, (c + 1) * CHUNK)
             h_codes, h_scales = hidden[c]
-            bank = psum.tile([P, PACK, CHUNK], F32, name="out_bank_%d" % c)
+            bank = psum.tile([P, PACK, CHUNK], F32, name="out_bank_%d" % c, tag="out_bank_%d" % c)
             for t in range(PACK):
                 m_cols = slice(t * P, (t + 1) * P)
                 nc.tensor.matmul_mx(
@@ -180,20 +208,33 @@ def tile_picked_zlayout_silu_po_kernel(
                     stop=True,
                 )
             result[c] = keep.tile([P, PACK, CHUNK], F32, name="result_%d" % c, align_bytes=64)
-            nc.scalar.copy(result[c][:], bank[:])
+            copy_out = nc.vector.tensor_copy if c == 1 else nc.scalar.copy
+            copy_out(result[c][:], bank[:])
             nc.sync.dma_start(out=out_rows[:, :, cols], in_=result[c][:])
-            out_bf16 = keep.tile([P, CHUNK, PACK], BF16, name="out_bf16_%d" % c, align_bytes=64)
-            nc.vector.tensor_copy(out_bf16[:], result[c][:].rearrange("p t n -> p n t"))
-            nc.vector.quantize_mx(out=out_words[:, cols].bitcast(FP8X4), scales=out_scales[:, cols], in_=out_bf16[:].rearrange("p n t -> p (n t)"))
-            if c % 2 == 1:
-                half = slice((c - 1) * CHUNK, (c + 1) * CHUNK)
-                nc.sync.dma_start(out=words_view(out_1)[:, half], in_=out_words[:, half])
 
-        for c in range(CHUNKS + 2):
-            if c < CHUNKS:
-                first_product(c)
-            if c >= 2:
-                second_product(c - 2)
+        def round_result(c):
+            nc.vector.tensor_copy(out_bf16[:, c * CHUNK : (c + 1) * CHUNK, :], result[c][:].rearrange("p t n -> p n t"))
+
+        def quantize_result(c0, c1):
+            cols = slice(c0 * CHUNK, c1 * CHUNK)
+            nc.vector.quantize_mx(out=out_words[:, cols].bitcast(FP8X4), scales=out_scales[:, cols], in_=out_bf16[:, cols, :].rearrange("p n t -> p (n t)"))
+
+        def store_words(c0, c1):
+            cols = slice(c0 * CHUNK, c1 * CHUNK)
+            nc.sync.dma_start(out=words_view(out_1)[:, cols], in_=out_words[:, cols])
+
+        out_bf16 = keep.tile([P, S, PACK], BF16, name="out_bf16", align_bytes=64)
+        for c in range(CHUNKS):
+            first_product(c)
+        for c in range(CHUNKS):
+            second_product(c)
+        for c in range(CHUNKS):
+            round_result(c)
+        quantize_result(0, 2)
+        store_words(0, 2)
+        quantize_result(2, 3)
+        quantize_result(3, 4)
+        store_words(2, 4)
 
         for q in range(4):
             queue = nc.sync if q % 2 == 0 else nc.scalar

@@ -51,9 +51,9 @@ def tile_picked_zlayout_silu_po_kernel(
         nc.gpsimd.memset(w4_plane[:].bitcast(I32), 0)
         nc.vector.memset(plane["x"][:].bitcast(I32), 0)
 
-        def load_scales(tile, scales, first, quadrants):
-            for q in quadrants:
-                nc.sync.dma_start(out=tile[32 * q + first : 32 * q + first + 4, :].bitcast(I32), in_=scales[0, 4 * q : 4 * q + 4, :].bitcast(I32))
+        def load_scales(tile, scales, first, rows):
+            for r in rows:
+                nc.sync.dma_start(out=tile[first + r : P : 32, :].bitcast(I32), in_=scales[0, r:16:4, :].bitcast(I32))
 
         raw, lists, table = {}, {}, {}
 
@@ -208,7 +208,7 @@ def tile_picked_zlayout_silu_po_kernel(
                     stop=True,
                 )
             result[c] = keep.tile([P, PACK, CHUNK], F32, name="result_%d" % c, align_bytes=64)
-            copy_out = nc.vector.tensor_copy if c == 1 else nc.scalar.copy
+            copy_out = nc.vector.tensor_copy if c < 2 else nc.scalar.copy
             copy_out(result[c][:], bank[:])
             nc.sync.dma_start(out=out_rows[:, :, cols], in_=result[c][:])
 
@@ -224,9 +224,11 @@ def tile_picked_zlayout_silu_po_kernel(
             nc.sync.dma_start(out=words_view(out_1)[:, cols], in_=out_words[:, cols])
 
         out_bf16 = keep.tile([P, S, PACK], BF16, name="out_bf16", align_bytes=64)
-        for c in range(CHUNKS):
+        for c in range(CHUNKS - 1):
             first_product(c)
-        for c in range(CHUNKS):
+        second_product(0)
+        first_product(CHUNKS - 1)
+        for c in range(1, CHUNKS):
             second_product(c)
         for c in range(CHUNKS):
             round_result(c)
@@ -238,4 +240,4 @@ def tile_picked_zlayout_silu_po_kernel(
 
         for q in range(4):
             queue = nc.sync if q % 2 == 0 else nc.scalar
-            queue.dma_start(out=out_2[0, 4 * q : 4 * q + 4, :].bitcast(I32), in_=out_scales[32 * q : 32 * q + 4, :].bitcast(I32))
+            queue.dma_start(out=out_2[0, q:16:4, :].bitcast(I32), in_=out_scales[q:P:32, :].bitcast(I32))

@@ -22,6 +22,7 @@ LIST_COLS = S // 16
 WARM = 4
 TABLE_AT = {"x": 0, "y": 4 * T, "e": 4 * (T + W)}
 PLANE_X_AT = 4 * (T + 2 * W)
+PLANE_Y_AT = PLANE_X_AT + T + H
 
 
 def tile_picked_zlayout_silu_po_kernel(
@@ -42,18 +43,17 @@ def tile_picked_zlayout_silu_po_kernel(
 
         plane = {}
         plane["x"] = reused.tile([P, T], U8, name="plane_x", align_bytes=64, offset=PLANE_X_AT)
-        for name in ("e", "y"):
-            plane[name] = keep.tile([P, tables[name][3]], U8, name="plane_" + name, align_bytes=64)
+        plane["y"] = reused.tile([P, W], U8, name="plane_y", align_bytes=64, offset=PLANE_Y_AT)
+        plane["e"] = keep.tile([P, W], U8, name="plane_e", align_bytes=64)
         w4_plane = keep.tile([P, N], U8, name="w4_plane", align_bytes=64)
-        nc.vector.memset(plane["e"][:, : W // 2].bitcast(I32), 0)
-        nc.gpsimd.memset(plane["e"][:, W // 2 :].bitcast(I32), 0)
+        nc.vector.memset(plane["e"][:].bitcast(I32), 0)
+        nc.gpsimd.memset(plane["x"][:].bitcast(I32), 0)
         nc.vector.memset(plane["y"][:].bitcast(I32), 0)
-        nc.gpsimd.memset(w4_plane[:].bitcast(I32), 0)
-        nc.vector.memset(plane["x"][:].bitcast(I32), 0)
+        nc.vector.memset(w4_plane[:].bitcast(I32), 0)
 
-        def load_scales(tile, scales, first, rows):
-            for r in rows:
-                nc.sync.dma_start(out=tile[first + r : P : 32, :].bitcast(I32), in_=scales[0, r:16:4, :].bitcast(I32))
+        def load_scales(queue, tile, scales, first):
+            for r in range(4):
+                queue.dma_start(out=tile[first + r : P : 32, :].bitcast(I32), in_=scales[0, r:16:4, :].bitcast(I32))
 
         raw, lists, table = {}, {}, {}
 
@@ -69,18 +69,17 @@ def tile_picked_zlayout_silu_po_kernel(
             table[name] = reused.tile([P, tables[name][3]], I32, name="table_" + name, align_bytes=64, offset=TABLE_AT[name])
             nc.sync.dma_start(out=table[name][:], in_=words_view(tables[name][0]))
 
+        load_scales(nc.gpsimd, plane["x"], x_scales, tables["x"][4])
         load_list("e")
         load_table("e")
-        load_list("x")
         load_list("y")
-        load_scales(plane["e"], e_scales, tables["e"][4], range(0, 3))
+        load_scales(nc.sync, plane["e"], e_scales, tables["e"][4])
         load_w("x", w1)
-        load_scales(plane["e"], e_scales, tables["e"][4], range(3, 4))
-        load_scales(plane["y"], y_scales, tables["y"][4], range(4))
+        load_list("x")
+        load_scales(nc.sync, plane["y"], y_scales, tables["y"][4])
         load_w("e", w2)
-        load_scales(plane["x"], x_scales, tables["x"][4], range(4))
         load_w("y", w3)
-        load_scales(w4_plane, w4_scales, W4_ROW, range(4))
+        load_scales(nc.sync, w4_plane, w4_scales, W4_ROW)
         load_table("x")
         load_table("y")
         w4_raw = keep.tile([P, N], I32, name="w4_raw", align_bytes=64)
@@ -89,7 +88,10 @@ def tile_picked_zlayout_silu_po_kernel(
         picked_scales, picked = {}, {}
 
         def gather_scales(name):
-            picked_scales[name] = keep.tile([P, S], U8, name="picked_scales_" + name, align_bytes=64)
+            if name == "x":
+                picked_scales[name] = reused.tile([P, S], U8, name="picked_scales_" + name, align_bytes=64, offset=PLANE_Y_AT)
+            else:
+                picked_scales[name] = keep.tile([P, S], U8, name="picked_scales_" + name, align_bytes=64)
             nc.vector.tensor_copy(picked_scales[name][:], plane[name][:].indirect(lists[name][:]))
 
         def gather_words(name, c0, c1):
@@ -105,8 +107,8 @@ def tile_picked_zlayout_silu_po_kernel(
         grouped, w_codes, w_scales = {}, {}, {}
 
         def round_w(name, copy, t0, t1):
-            if (name, t0) == ("y", 2):
-                grouped[name, t0] = reused.tile([P, t1 - t0, P, PACK], BF16, name="grouped_%s_%d" % (name, t0), align_bytes=64, offset=PLANE_X_AT + H)
+            if t0 == 2:
+                grouped[name, t0] = reused.tile([P, t1 - t0, P, PACK], BF16, name="grouped_%s_%d" % (name, t0), align_bytes=64, offset=PLANE_Y_AT + S if name == "x" else PLANE_X_AT + H)
             else:
                 grouped[name, t0] = keep.tile([P, t1 - t0, P, PACK], BF16, name="grouped_%s_%d" % (name, t0), align_bytes=64)
             copy(
@@ -128,9 +130,11 @@ def tile_picked_zlayout_silu_po_kernel(
         picked_e = gather_words("e", 0, S)
         gather_scales("e")
         gather_scales("y")
-        round_w("x", nc.scalar.copy, 0, PACK)
+        round_w("x", nc.scalar.copy, 0, 2)
+        round_w("x", nc.vector.tensor_copy, 2, PACK)
+        quantize_w("x", 0, 2)
+        quantize_w("x", 2, PACK)
         gather_scales("x")
-        quantize_w("x", 0, PACK)
         round_w("e", nc.scalar.copy, 0, PACK)
         quantize_w("e", 0, PACK)
         round_w("y", nc.scalar.copy, 0, 2)

@@ -16,13 +16,16 @@ SILU = mybir.ActivationFunctionType.Silu
 
 P = 128
 PACK = 4
+PAIR = 2
 CHUNK = 128
 CHUNKS = S // CHUNK
 LIST_COLS = S // 16
-WARM = 4
-TABLE_AT = {"x": 0, "y": 4 * T, "e": 4 * (T + W)}
-PLANE_X_AT = 4 * (T + 2 * W)
-PLANE_Y_AT = PLANE_X_AT + T + H
+HALF_BYTES = PAIR * P * PACK * 2
+TABLE_X_AT = 0
+PLANE_X_AT = 4 * T
+W2_AT = PLANE_X_AT + H + 2 * HALF_BYTES
+W1_LOW_AT = W2_AT + 2 * HALF_BYTES + 4 * S
+PICKED_AT = {"x": W1_LOW_AT - 4 * S + 64}
 
 
 def tile_picked_zlayout_silu_po_kernel(
@@ -35,6 +38,11 @@ def tile_picked_zlayout_silu_po_kernel(
         reused = ctx.enter_context(tc.tile_pool(name="reused", bufs=1))
         psum = ctx.enter_context(tc.psum_pool(name="psum", bufs=1))
 
+        def sbuf_tile(shape, dtype, name, at=None):
+            if at is None:
+                return keep.tile(shape, dtype, name=name, align_bytes=64)
+            return reused.tile(shape, dtype, name=name, align_bytes=64, offset=at)
+
         def words_view(words):
             return words[0].rearrange("p n t -> p (n t)").bitcast(I32)
 
@@ -42,13 +50,13 @@ def tile_picked_zlayout_silu_po_kernel(
         W4_ROW = 12
 
         plane = {}
-        plane["x"] = reused.tile([P, T], U8, name="plane_x", align_bytes=64, offset=PLANE_X_AT)
-        plane["y"] = reused.tile([P, W], U8, name="plane_y", align_bytes=64, offset=PLANE_Y_AT)
-        plane["e"] = keep.tile([P, W], U8, name="plane_e", align_bytes=64)
-        w4_plane = keep.tile([P, N], U8, name="w4_plane", align_bytes=64)
+        plane["x"] = sbuf_tile([P, T], U8, "plane_x", PLANE_X_AT)
+        plane["y"] = sbuf_tile([P, W], U8, "plane_y")
+        plane["e"] = sbuf_tile([P, W], U8, "plane_e")
+        w4_plane = sbuf_tile([P, N], U8, "w4_plane")
         nc.vector.memset(plane["e"][:].bitcast(I32), 0)
-        nc.gpsimd.memset(plane["x"][:].bitcast(I32), 0)
         nc.vector.memset(plane["y"][:].bitcast(I32), 0)
+        nc.vector.memset(plane["x"][:].bitcast(I32), 0)
         nc.vector.memset(w4_plane[:].bitcast(I32), 0)
 
         def load_scales(queue, tile, scales, first):
@@ -58,162 +66,169 @@ def tile_picked_zlayout_silu_po_kernel(
         raw, lists, table = {}, {}, {}
 
         def load_w(name, w):
-            raw[name] = keep.tile([P, PACK, H], F32, name="raw_" + name)
+            raw[name] = sbuf_tile([P, PACK, H], F32, "raw_" + name)
             nc.sync.dma_start(out=raw[name][:], in_=w.rearrange("(p j) c -> p j c", j=PACK))
 
         def load_list(name):
             lists[name] = keep.tile([P, LIST_COLS], U16, name="list_" + name)
             nc.sync.dma_start(lists[name][:], tables[name][2])
 
-        def load_table(name):
-            table[name] = reused.tile([P, tables[name][3]], I32, name="table_" + name, align_bytes=64, offset=TABLE_AT[name])
+        def load_table(name, at=None):
+            table[name] = sbuf_tile([P, tables[name][3]], I32, "table_" + name, at)
             nc.sync.dma_start(out=table[name][:], in_=words_view(tables[name][0]))
 
-        load_scales(nc.gpsimd, plane["x"], x_scales, tables["x"][4])
-        load_list("e")
         load_table("e")
+        load_list("e")
         load_list("y")
         load_scales(nc.sync, plane["e"], e_scales, tables["e"][4])
-        load_w("x", w1)
-        load_list("x")
-        load_scales(nc.sync, plane["y"], y_scales, tables["y"][4])
         load_w("e", w2)
-        load_w("y", w3)
-        load_scales(nc.sync, w4_plane, w4_scales, W4_ROW)
-        load_table("x")
+        load_scales(nc.sync, plane["y"], y_scales, tables["y"][4])
+        load_list("x")
         load_table("y")
-        w4_raw = keep.tile([P, N], I32, name="w4_raw", align_bytes=64)
+        load_w("y", w3)
+        load_scales(nc.sync, plane["x"], x_scales, tables["x"][4])
+        load_w("x", w1)
+        load_scales(nc.sync, w4_plane, w4_scales, W4_ROW)
+        load_table("x", TABLE_X_AT)
+        w4_raw = sbuf_tile([P, N], I32, "w4_raw")
         nc.sync.dma_start(out=w4_raw[:], in_=words_view(w4_words))
 
         picked_scales, picked = {}, {}
 
-        def gather_scales(name):
-            if name == "x":
-                picked_scales[name] = reused.tile([P, S], U8, name="picked_scales_" + name, align_bytes=64, offset=PLANE_Y_AT)
-            else:
-                picked_scales[name] = keep.tile([P, S], U8, name="picked_scales_" + name, align_bytes=64)
+        def gather_scales(name, at=None):
+            picked_scales[name] = sbuf_tile([P, S], U8, "picked_scales_" + name, at)
             nc.vector.tensor_copy(picked_scales[name][:], plane[name][:].indirect(lists[name][:]))
 
-        def gather_words(name, c0, c1):
-            if name == "y":
-                piece = reused.tile([P, c1 - c0], U32, name="picked_%s_%d" % (name, c0), align_bytes=64, offset=TABLE_AT["x"] + 4 * c0)
-            else:
-                piece = keep.tile([P, c1 - c0], U32, name="picked_%s_%d" % (name, c0), align_bytes=64)
-            nc.vector.tensor_copy(piece[:], table[name][:].bitcast(U32).indirect(lists[name][:, c0 // 16 : c1 // 16]))
-            for c in range(c0 // CHUNK, c1 // CHUNK):
-                picked[name, c] = piece[:, c * CHUNK - c0 : (c + 1) * CHUNK - c0]
-            return piece
+        def gather_words(name, pieces):
+            picked[name] = sbuf_tile([P, S], U32, "picked_" + name, PICKED_AT.get(name))
+            width = S // pieces
+            for c0 in range(0, S, width):
+                window = table[name][:].bitcast(U32)
+                nc.vector.tensor_copy(picked[name][:, c0 : c0 + width], window.indirect(lists[name][:, c0 // 16 : (c0 + width) // 16]))
 
         grouped, w_codes, w_scales = {}, {}, {}
 
-        def round_w(name, copy, t0, t1):
-            if t0 == 2:
-                grouped[name, t0] = reused.tile([P, t1 - t0, P, PACK], BF16, name="grouped_%s_%d" % (name, t0), align_bytes=64, offset=PLANE_Y_AT + S if name == "x" else PLANE_X_AT + H)
-            else:
-                grouped[name, t0] = keep.tile([P, t1 - t0, P, PACK], BF16, name="grouped_%s_%d" % (name, t0), align_bytes=64)
+        def round_w(name, copy, t0, t1, at=None):
+            grouped[name, t0] = sbuf_tile([P, t1 - t0, P, PACK], BF16, "grouped_%s_%d" % (name, t0), at)
             copy(
                 grouped[name, t0][:].rearrange("p t m j -> p m j t"),
                 raw[name][:].rearrange("p j (m t) -> p m j t", t=PACK)[:, :, :, t0:t1],
             )
 
-        def quantize_w(name, t0, t1):
-            codes = keep.tile([P, (t1 - t0) * P], U32, name="w_codes_%s_%d" % (name, t0), align_bytes=64)
-            if name == "e":
-                scales = reused.tile([P, (t1 - t0) * P], U8, name="w_scales_%s_%d" % (name, t0), align_bytes=64, offset=PLANE_X_AT)
-            else:
-                scales = keep.tile([P, (t1 - t0) * P], U8, name="w_scales_%s_%d" % (name, t0), align_bytes=64)
+        def quantize_w(name, t0, t1, at=None):
+            codes = sbuf_tile([P, (t1 - t0) * P], U32, "w_codes_%s_%d" % (name, t0))
+            scales = sbuf_tile([P, (t1 - t0) * P], U8, "w_scales_%s_%d" % (name, t0), at)
             nc.vector.quantize_mx(out=codes[:].bitcast(FP8X4), scales=scales[:], in_=grouped[name, t0][:].rearrange("p t m j -> p (t m j)"))
             for t in range(t0, t1):
                 w_codes[name, t] = codes[:, (t - t0) * P : (t - t0 + 1) * P]
                 w_scales[name, t] = scales[:, (t - t0) * P : (t - t0 + 1) * P]
 
-        picked_e = gather_words("e", 0, S)
+        gather_words("e", 1)
         gather_scales("e")
         gather_scales("y")
-        round_w("x", nc.scalar.copy, 0, 2)
-        round_w("x", nc.vector.tensor_copy, 2, PACK)
-        quantize_w("x", 0, 2)
-        quantize_w("x", 2, PACK)
-        gather_scales("x")
-        round_w("e", nc.scalar.copy, 0, PACK)
+        gather_words("y", 1)
+        round_w("e", nc.scalar.copy, 0, PACK, W2_AT)
         quantize_w("e", 0, PACK)
-        round_w("y", nc.scalar.copy, 0, 2)
-        round_w("y", nc.vector.tensor_copy, 2, PACK)
-        quantize_w("y", 0, 2)
-        quantize_w("y", 2, PACK)
-        gather_words("x", 0, S // 2)
-        gather_words("x", S // 2, S)
-        h_banks = [psum.tile([P, PACK, CHUNK], F32, name="h_bank_%d" % c) for c in range(CHUNKS)]
+        gather_scales("x", W2_AT)
+        round_w("y", nc.scalar.copy, 0, PACK)
+        round_w("x", nc.scalar.copy, 0, PAIR, W1_LOW_AT)
+        round_w("x", nc.vector.tensor_copy, PAIR, PACK, PLANE_X_AT + 2 * H)
+        quantize_w("y", 0, PACK, PLANE_X_AT)
+        quantize_w("x", PAIR, PACK)
+        quantize_w("x", 0, PAIR)
+        gather_words("x", 2)
+        w4_dealt_scales = sbuf_tile([P, N], U8, "w4_dealt_scales", TABLE_X_AT + 4 * N)
+        nc.vector.tensor_copy(w4_dealt_scales[:].rearrange("p (t m) -> p m t", t=PACK), w4_plane[:].rearrange("p (m t) -> p m t", t=PACK))
+        w4_dealt = sbuf_tile([P, N], I32, "w4_dealt", TABLE_X_AT)
+        nc.vector.tensor_copy(w4_dealt[:].rearrange("p (t m) -> p m t", t=PACK), w4_raw[:].rearrange("p (m t) -> p m t", t=PACK))
 
-        def first_pass(c, t, name):
-            nc.tensor.matmul_mx(
-                out=h_banks[c][:, t, :],
-                lhsT=w_codes[name, t].bitcast(FP8X4),
-                lhsT_scale=w_scales[name, t],
-                rhs=picked[name, c].bitcast(FP8X4),
-                rhs_scale=picked_scales[name][tables[name][4] :, c * CHUNK : (c + 1) * CHUNK],
-                start=(name == "e"),
-                stop=(name == "y"),
-            )
+        def bank_tag(c, u):
+            return "bank_%d_%d" % (c, u)
 
-        for c in range(CHUNKS):
-            first_pass(c, 0, "e")
-        for t in range(WARM):
-            warm = psum.tile([P, S], F32, name="warm", tag="out_bank_%d" % t)
+        def warm_up(name, t, scales, c, u):
+            warm = psum.tile([P, S], F32, name="warm_%d_%d" % (c, u), tag=bank_tag(c, u))
             nc.tensor.matmul_mx(
                 out=warm[:],
-                lhsT=w_codes["e", t].bitcast(FP8X4),
-                lhsT_scale=w_scales["e", t],
-                rhs=picked_e[:].bitcast(FP8X4),
-                rhs_scale=picked_scales["e"][tables["e"][4] :, :],
+                lhsT=w_codes[name, t].bitcast(FP8X4),
+                lhsT_scale=w_scales[name, t],
+                rhs=picked["e"][:].bitcast(FP8X4),
+                rhs_scale=picked_scales[scales][tables[scales][4] :, :],
                 start=True,
                 stop=True,
             )
-        for c in range(CHUNKS):
-            first_pass(c, 0, "x")
-        for c in range(CHUNKS):
-            gather_words("y", c * CHUNK, (c + 1) * CHUNK)
-        w4_dealt_scales = reused.tile([P, N], U8, name="w4_dealt_scales", align_bytes=64, offset=TABLE_AT["y"] + 4 * N)
-        nc.vector.tensor_copy(w4_dealt_scales[:].rearrange("p (t m) -> p m t", t=PACK), w4_plane[:].rearrange("p (m t) -> p m t", t=PACK))
-        w4_dealt = reused.tile([P, N], I32, name="w4_dealt", align_bytes=64, offset=TABLE_AT["y"])
-        nc.vector.tensor_copy(w4_dealt[:].rearrange("p (t m) -> p m t", t=PACK), w4_raw[:].rearrange("p (m t) -> p m t", t=PACK))
 
-        out_words = keep.tile([P, S], I32, name="out_words", align_bytes=64)
-        out_scales = keep.tile([P, S], U8, name="out_scales", align_bytes=64)
+        warm_up("e", 0, "e", 1, 1)
+        warm_up("e", 1, "x", 2, 1)
+        warm_up("e", 2, "x", 3, 0)
+        warm_up("y", 0, "x", 3, 1)
+        h_banks = {}
+        for c in range(CHUNKS):
+            for u in range(PAIR):
+                h_banks[c, u] = psum.tile([P, PAIR, CHUNK], F32, name="h_bank_%d_%d" % (c, u), tag=bank_tag(c, u))
+
+        def first_pass(c, t, name):
+            cols = slice(c * CHUNK, (c + 1) * CHUNK)
+            nc.tensor.matmul_mx(
+                out=h_banks[c, t // PAIR][:, t % PAIR, :],
+                lhsT=w_codes[name, t].bitcast(FP8X4),
+                lhsT_scale=w_scales[name, t],
+                rhs=picked[name][:, cols].bitcast(FP8X4),
+                rhs_scale=picked_scales[name][tables[name][4] :, cols],
+                start=(name == "e"),
+                stop=(name == "x"),
+            )
+
+        for name in ("e", "y"):
+            for c in range(CHUNKS):
+                for u in range(PAIR):
+                    first_pass(c, PAIR * u, name)
+
+        out_words = sbuf_tile([P, S], I32, "out_words")
+        out_scales = sbuf_tile([P, S], U8, "out_scales")
+        out_bf16 = sbuf_tile([P, S, PACK], BF16, "out_bf16")
         out_rows = out_0.rearrange("(p t) j -> p t j", t=PACK)
-        hidden, result = {}, {}
+        hidden, result, h_tiles = {}, {}, {}
 
-        def first_product(c):
-            bank = h_banks[c]
-            first_pass(c, 0, "y")
-            for t in range(1, PACK):
-                for name in ("e", "x", "y"):
-                    first_pass(c, t, name)
-            h_bf16 = keep.tile([P, CHUNK, PACK], BF16, name="h_bf16_%d" % c, align_bytes=64)
-            nc.scalar.activation(h_bf16[:], bank[:].rearrange("p t n -> p n t"), SILU)
-            h_codes = keep.tile([P, CHUNK], U32, name="h_codes_%d" % c, align_bytes=64)
-            h_scales = keep.tile([P, CHUNK], U8, name="h_scales_%d" % c, align_bytes=64)
+        def first_product(c, direct):
+            h_bf16 = sbuf_tile([P, CHUNK, PACK], BF16, "h_bf16_%d" % c)
+            h_pairs = None if direct else sbuf_tile([P, PAIR, CHUNK, PAIR], BF16, "h_pairs_%d" % c)
+            for u in range(PAIR):
+                first_pass(c, PAIR * u, "x")
+                for name in ("e", "y", "x"):
+                    first_pass(c, PAIR * u + 1, name)
+                target = h_bf16[:, :, PAIR * u : PAIR * u + PAIR] if direct else h_pairs[:, u, :, :]
+                nc.scalar.activation(target, h_banks[c, u][:].rearrange("p t n -> p n t"), SILU)
+            if not direct:
+                nc.vector.tensor_copy(
+                    h_bf16[:].rearrange("p n t -> p (n t)").bitcast(I32).rearrange("p (n u) -> p n u", u=PAIR),
+                    h_pairs[:].rearrange("p u n t -> p (u n t)").bitcast(I32).rearrange("p (u n) -> p n u", u=PAIR),
+                )
+            h_codes = sbuf_tile([P, CHUNK], U32, "h_codes_%d" % c)
+            h_scales = sbuf_tile([P, CHUNK], U8, "h_scales_%d" % c)
             nc.vector.quantize_mx(out=h_codes[:].bitcast(FP8X4), scales=h_scales[:], in_=h_bf16[:].rearrange("p n t -> p (n t)"))
             hidden[c] = (h_codes, h_scales)
+            h_tiles[c] = h_bf16
+            h_tiles[c, 0] = h_pairs
 
-        def second_product(c):
+        def second_product(c, copies):
             cols = slice(c * CHUNK, (c + 1) * CHUNK)
             h_codes, h_scales = hidden[c]
-            bank = psum.tile([P, PACK, CHUNK], F32, name="out_bank_%d" % c, tag="out_bank_%d" % c)
-            for t in range(PACK):
-                m_cols = slice(t * P, (t + 1) * P)
-                nc.tensor.matmul_mx(
-                    out=bank[:, t, :],
-                    lhsT=w4_dealt[:, m_cols].bitcast(FP8X4),
-                    lhsT_scale=w4_dealt_scales[W4_ROW:, m_cols],
-                    rhs=h_codes[:].bitcast(FP8X4),
-                    rhs_scale=h_scales[:],
-                    start=True,
-                    stop=True,
-                )
-            result[c] = keep.tile([P, PACK, CHUNK], F32, name="result_%d" % c, align_bytes=64)
-            copy_out = nc.vector.tensor_copy if c < 2 else nc.scalar.copy
-            copy_out(result[c][:], bank[:])
+            result[c] = sbuf_tile([P, PACK, CHUNK], F32, "result_%d" % c)
+            share = PACK // len(copies)
+            for u, copy_out in enumerate(copies):
+                bank = psum.tile([P, share, CHUNK], F32, name="out_bank_%d_%d" % (c, u), tag=bank_tag(c, u))
+                for i in range(share):
+                    m_cols = slice((u * share + i) * P, (u * share + i + 1) * P)
+                    nc.tensor.matmul_mx(
+                        out=bank[:, i, :],
+                        lhsT=w4_dealt[:, m_cols].bitcast(FP8X4),
+                        lhsT_scale=w4_dealt_scales[W4_ROW:, m_cols],
+                        rhs=h_codes[:].bitcast(FP8X4),
+                        rhs_scale=h_scales[:],
+                        start=True,
+                        stop=True,
+                    )
+                copy_out(result[c][:, u * share : (u + 1) * share, :], bank[:])
             nc.sync.dma_start(out=out_rows[:, :, cols], in_=result[c][:])
 
         def round_result(c):
@@ -227,17 +242,20 @@ def tile_picked_zlayout_silu_po_kernel(
             cols = slice(c0 * CHUNK, c1 * CHUNK)
             nc.sync.dma_start(out=words_view(out_1)[:, cols], in_=out_words[:, cols])
 
-        out_bf16 = keep.tile([P, S, PACK], BF16, name="out_bf16", align_bytes=64)
-        for c in range(CHUNKS - 1):
-            first_product(c)
-        second_product(0)
-        first_product(CHUNKS - 1)
-        for c in range(1, CHUNKS):
-            second_product(c)
-        for c in range(CHUNKS):
-            round_result(c)
+        first_product(0, False)
+        first_product(1, False)
+        first_product(2, False)
+        first_product(3, False)
+        second_product(0, [nc.scalar.copy])
+        second_product(1, [nc.scalar.copy])
+        second_product(2, [nc.scalar.copy])
+        second_product(3, [nc.scalar.copy, nc.vector.tensor_copy])
+        round_result(0)
+        round_result(1)
         quantize_result(0, 2)
         store_words(0, 2)
+        round_result(2)
+        round_result(3)
         quantize_result(2, 3)
         quantize_result(3, 4)
         store_words(2, 4)

@@ -138,9 +138,9 @@ def tile_picked_zlayout_silu_po_kernel(
         quantize_w("x", 0, PAIR)
         gather_words("x", 2)
         w4_dealt_scales = sbuf_tile([P, N], U8, "w4_dealt_scales", TABLE_X_AT + 4 * N)
-        nc.vector.tensor_copy(w4_dealt_scales[:].rearrange("p (t m) -> p m t", t=PACK), w4_plane[:].rearrange("p (m t) -> p m t", t=PACK))
+        nc.vector.tensor_copy(w4_dealt_scales[:].rearrange("p (t g i) -> p g t i", t=PACK, i=16), w4_plane[:].rearrange("p (g i t) -> p g t i", t=PACK, i=16))
         w4_dealt = sbuf_tile([P, N], I32, "w4_dealt", TABLE_X_AT)
-        nc.vector.tensor_copy(w4_dealt[:].rearrange("p (t m) -> p m t", t=PACK), w4_raw[:].rearrange("p (m t) -> p m t", t=PACK))
+        nc.vector.tensor_copy(w4_dealt[:].rearrange("p (t g i) -> p g t i", t=PACK, i=4), w4_raw[:].rearrange("p (g i t) -> p g t i", t=PACK, i=4))
 
         def bank_tag(c, u):
             return "bank_%d_%d" % (c, u)

@@ -232,7 +232,10 @@ def tile_picked_zlayout_silu_po_kernel(
             nc.sync.dma_start(out=out_rows[:, :, cols], in_=result[c][:])
 
         def round_result(c):
-            nc.vector.tensor_copy(out_bf16[:, c * CHUNK : (c + 1) * CHUNK, :], result[c][:].rearrange("p t n -> p n t"))
+            nc.vector.tensor_copy(
+                out_bf16[:, c * CHUNK : (c + 1) * CHUNK, :].rearrange("p (g i) t -> p g t i", i=4),
+                result[c][:].rearrange("p t (g i) -> p g t i", i=4),
+            )
 
         def quantize_result(c0, c1):
             cols = slice(c0 * CHUNK, c1 * CHUNK)

@@ -19,13 +19,21 @@ PACK = 4
 PAIR = 2
 CHUNK = 128
 CHUNKS = S // CHUNK
-LIST_COLS = S // 16
-HALF_BYTES = PAIR * P * PACK * 2
+GROUP = 16
+LINE = 16
+ALIGN = 64
+X_PIECES = 2
+
+FIRST_ROW = {"x": 0, "e": 4, "y": 8, "w4": 12}
+
+PAIR_BYTES = PAIR * P * PACK * 2
 TABLE_X_AT = 0
+W4_SCALES_AT = TABLE_X_AT + 4 * N
 PLANE_X_AT = 4 * T
-W2_AT = PLANE_X_AT + H + 2 * HALF_BYTES
-W1_LOW_AT = W2_AT + 2 * HALF_BYTES + 4 * S
-PICKED_AT = {"x": W1_LOW_AT - 4 * S + 64}
+W1_HIGH_AT = PLANE_X_AT + 2 * H
+W2_AT = PLANE_X_AT + H + 2 * PAIR_BYTES
+W1_LOW_AT = W2_AT + 2 * PAIR_BYTES + 4 * S
+PICKED_X_AT = W1_LOW_AT - 4 * S + ALIGN
 
 
 def tile_picked_zlayout_silu_po_kernel(
@@ -35,60 +43,61 @@ def tile_picked_zlayout_silu_po_kernel(
     nc = tc.nc
     with ExitStack() as ctx:
         keep = ctx.enter_context(tc.tile_pool(name="keep", bufs=1))
-        reused = ctx.enter_context(tc.tile_pool(name="reused", bufs=1))
+        shared = ctx.enter_context(tc.tile_pool(name="shared", bufs=1))
         psum = ctx.enter_context(tc.psum_pool(name="psum", bufs=1))
 
         def sbuf_tile(shape, dtype, name, at=None):
             if at is None:
-                return keep.tile(shape, dtype, name=name, align_bytes=64)
-            return reused.tile(shape, dtype, name=name, align_bytes=64, offset=at)
+                return keep.tile(shape, dtype, name=name, align_bytes=ALIGN)
+            return shared.tile(shape, dtype, name=name, align_bytes=ALIGN, offset=at)
 
         def words_view(words):
             return words[0].rearrange("p n t -> p (n t)").bitcast(I32)
 
-        tables = {"e": (e_words, e_scales, tok, W, 4), "x": (x_words, x_scales, offs, T, 0), "y": (y_words, y_scales, row, W, 8)}
-        W4_ROW = 12
+        words_in = {"e": e_words, "x": x_words, "y": y_words}
+        scales_in = {"e": e_scales, "x": x_scales, "y": y_scales, "w4": w4_scales}
+        list_in = {"e": tok, "x": offs, "y": row}
+        weight_in = {"e": w2, "x": w1, "y": w3}
+        columns = {"e": W, "x": T, "y": W}
 
         plane = {}
         plane["x"] = sbuf_tile([P, T], U8, "plane_x", PLANE_X_AT)
         plane["y"] = sbuf_tile([P, W], U8, "plane_y")
         plane["e"] = sbuf_tile([P, W], U8, "plane_e")
-        w4_plane = sbuf_tile([P, N], U8, "w4_plane")
-        nc.vector.memset(plane["e"][:].bitcast(I32), 0)
-        nc.vector.memset(plane["y"][:].bitcast(I32), 0)
-        nc.vector.memset(plane["x"][:].bitcast(I32), 0)
-        nc.vector.memset(w4_plane[:].bitcast(I32), 0)
-
-        def load_scales(queue, tile, scales, first):
-            for r in range(4):
-                queue.dma_start(out=tile[first + r : P : 32, :].bitcast(I32), in_=scales[0, r:16:4, :].bitcast(I32))
+        plane["w4"] = sbuf_tile([P, N], U8, "plane_w4")
+        for name in ("e", "y", "x", "w4"):
+            nc.vector.memset(plane[name][:].bitcast(I32), 0)
 
         raw, lists, table = {}, {}, {}
 
-        def load_w(name, w):
+        def load_scales(name):
+            for r in range(4):
+                nc.sync.dma_start(out=plane[name][FIRST_ROW[name] + r : P : 32, :].bitcast(I32), in_=scales_in[name][0, r:16:4, :].bitcast(I32))
+
+        def load_weight(name):
             raw[name] = sbuf_tile([P, PACK, H], F32, "raw_" + name)
-            nc.sync.dma_start(out=raw[name][:], in_=w.rearrange("(p j) c -> p j c", j=PACK))
+            nc.sync.dma_start(out=raw[name][:], in_=weight_in[name].rearrange("(p j) c -> p j c", j=PACK))
 
         def load_list(name):
-            lists[name] = keep.tile([P, LIST_COLS], U16, name="list_" + name)
-            nc.sync.dma_start(lists[name][:], tables[name][2])
+            lists[name] = keep.tile([P, S // GROUP], U16, name="list_" + name)
+            nc.sync.dma_start(lists[name][:], list_in[name])
 
         def load_table(name, at=None):
-            table[name] = sbuf_tile([P, tables[name][3]], I32, "table_" + name, at)
-            nc.sync.dma_start(out=table[name][:], in_=words_view(tables[name][0]))
+            table[name] = sbuf_tile([P, columns[name]], I32, "table_" + name, at)
+            nc.sync.dma_start(out=table[name][:], in_=words_view(words_in[name]))
 
         load_table("e")
         load_list("e")
         load_list("y")
-        load_scales(nc.sync, plane["e"], e_scales, tables["e"][4])
-        load_w("e", w2)
-        load_scales(nc.sync, plane["y"], y_scales, tables["y"][4])
+        load_scales("e")
+        load_weight("e")
+        load_scales("y")
         load_list("x")
         load_table("y")
-        load_w("y", w3)
-        load_scales(nc.sync, plane["x"], x_scales, tables["x"][4])
-        load_w("x", w1)
-        load_scales(nc.sync, w4_plane, w4_scales, W4_ROW)
+        load_weight("y")
+        load_scales("x")
+        load_weight("x")
+        load_scales("w4")
         load_table("x", TABLE_X_AT)
         w4_raw = sbuf_tile([P, N], I32, "w4_raw")
         nc.sync.dma_start(out=w4_raw[:], in_=words_view(w4_words))
@@ -99,60 +108,67 @@ def tile_picked_zlayout_silu_po_kernel(
             picked_scales[name] = sbuf_tile([P, S], U8, "picked_scales_" + name, at)
             nc.vector.tensor_copy(picked_scales[name][:], plane[name][:].indirect(lists[name][:]))
 
-        def gather_words(name, pieces):
-            picked[name] = sbuf_tile([P, S], U32, "picked_" + name, PICKED_AT.get(name))
+        def gather_words(name, pieces=1, at=None):
+            picked[name] = sbuf_tile([P, S], U32, "picked_" + name, at)
             width = S // pieces
             for c0 in range(0, S, width):
-                window = table[name][:].bitcast(U32)
-                nc.vector.tensor_copy(picked[name][:, c0 : c0 + width], window.indirect(lists[name][:, c0 // 16 : (c0 + width) // 16]))
+                offsets = lists[name][:, c0 // GROUP : (c0 + width) // GROUP]
+                nc.vector.tensor_copy(picked[name][:, c0 : c0 + width], table[name][:].bitcast(U32).indirect(offsets))
 
-        grouped, w_codes, w_scales = {}, {}, {}
+        rounded, w_codes, w_scales = {}, {}, {}
 
-        def round_w(name, copy, t0, t1, at=None):
-            grouped[name, t0] = sbuf_tile([P, t1 - t0, P, PACK], BF16, "grouped_%s_%d" % (name, t0), at)
+        def round_weight(name, copy, t0, t1, at=None):
+            rounded[name, t0] = sbuf_tile([P, t1 - t0, P, PACK], BF16, "rounded_%s_%d" % (name, t0), at)
             copy(
-                grouped[name, t0][:].rearrange("p t m j -> p m j t"),
+                rounded[name, t0][:].rearrange("p t m j -> p m j t"),
                 raw[name][:].rearrange("p j (m t) -> p m j t", t=PACK)[:, :, :, t0:t1],
             )
 
-        def quantize_w(name, t0, t1, at=None):
+        def quantize_weight(name, t0, t1, at=None):
             codes = sbuf_tile([P, (t1 - t0) * P], U32, "w_codes_%s_%d" % (name, t0))
             scales = sbuf_tile([P, (t1 - t0) * P], U8, "w_scales_%s_%d" % (name, t0), at)
-            nc.vector.quantize_mx(out=codes[:].bitcast(FP8X4), scales=scales[:], in_=grouped[name, t0][:].rearrange("p t m j -> p (t m j)"))
+            nc.vector.quantize_mx(out=codes[:].bitcast(FP8X4), scales=scales[:], in_=rounded[name, t0][:].rearrange("p t m j -> p (t m j)"))
             for t in range(t0, t1):
                 w_codes[name, t] = codes[:, (t - t0) * P : (t - t0 + 1) * P]
                 w_scales[name, t] = scales[:, (t - t0) * P : (t - t0 + 1) * P]
 
-        gather_words("e", 1)
+        gather_words("e")
         gather_scales("e")
         gather_scales("y")
-        gather_words("y", 1)
-        round_w("e", nc.scalar.copy, 0, PACK, W2_AT)
-        quantize_w("e", 0, PACK)
+        gather_words("y")
+        round_weight("e", nc.scalar.copy, 0, PACK, W2_AT)
+        quantize_weight("e", 0, PACK)
         gather_scales("x", W2_AT)
-        round_w("y", nc.scalar.copy, 0, PACK)
-        round_w("x", nc.scalar.copy, 0, PAIR, W1_LOW_AT)
-        round_w("x", nc.vector.tensor_copy, PAIR, PACK, PLANE_X_AT + 2 * H)
-        quantize_w("y", 0, PACK, PLANE_X_AT)
-        quantize_w("x", PAIR, PACK)
-        quantize_w("x", 0, PAIR)
-        gather_words("x", 2)
-        w4_dealt_scales = sbuf_tile([P, N], U8, "w4_dealt_scales", TABLE_X_AT + 4 * N)
-        nc.vector.tensor_copy(w4_dealt_scales[:].rearrange("p (t g i) -> p g t i", t=PACK, i=16), w4_plane[:].rearrange("p (g i t) -> p g t i", t=PACK, i=16))
+        round_weight("y", nc.scalar.copy, 0, PACK)
+        round_weight("x", nc.scalar.copy, 0, PAIR, W1_LOW_AT)
+        round_weight("x", nc.vector.tensor_copy, PAIR, PACK, W1_HIGH_AT)
+        quantize_weight("y", 0, PACK, PLANE_X_AT)
+        quantize_weight("x", PAIR, PACK)
+        quantize_weight("x", 0, PAIR)
+        gather_words("x", X_PIECES, PICKED_X_AT)
+
+        w4_dealt_scales = sbuf_tile([P, N], U8, "w4_dealt_scales", W4_SCALES_AT)
+        nc.vector.tensor_copy(
+            w4_dealt_scales[:].rearrange("p (t g i) -> p g t i", t=PACK, i=LINE),
+            plane["w4"][:].rearrange("p (g i t) -> p g t i", t=PACK, i=LINE),
+        )
         w4_dealt = sbuf_tile([P, N], I32, "w4_dealt", TABLE_X_AT)
-        nc.vector.tensor_copy(w4_dealt[:].rearrange("p (t g i) -> p g t i", t=PACK, i=4), w4_raw[:].rearrange("p (g i t) -> p g t i", t=PACK, i=4))
+        nc.vector.tensor_copy(
+            w4_dealt[:].rearrange("p (t g i) -> p g t i", t=PACK, i=LINE // 4),
+            w4_raw[:].rearrange("p (g i t) -> p g t i", t=PACK, i=LINE // 4),
+        )
 
         def bank_tag(c, u):
             return "bank_%d_%d" % (c, u)
 
-        def warm_up(name, t, scales, c, u):
+        def warm_up(weight, t, scales, c, u):
             warm = psum.tile([P, S], F32, name="warm_%d_%d" % (c, u), tag=bank_tag(c, u))
             nc.tensor.matmul_mx(
                 out=warm[:],
-                lhsT=w_codes[name, t].bitcast(FP8X4),
-                lhsT_scale=w_scales[name, t],
+                lhsT=w_codes[weight, t].bitcast(FP8X4),
+                lhsT_scale=w_scales[weight, t],
                 rhs=picked["e"][:].bitcast(FP8X4),
-                rhs_scale=picked_scales[scales][tables[scales][4] :, :],
+                rhs_scale=picked_scales[scales][FIRST_ROW[scales] :, :],
                 start=True,
                 stop=True,
             )
@@ -160,7 +176,7 @@ def tile_picked_zlayout_silu_po_kernel(
         warm_up("e", 0, "e", 1, 1)
         warm_up("e", 1, "x", 2, 1)
         warm_up("e", 2, "x", 3, 0)
-        warm_up("y", 0, "x", 3, 1)
+        warm_up("e", 3, "x", 3, 1)
         h_banks = {}
         for c in range(CHUNKS):
             for u in range(PAIR):
@@ -173,7 +189,7 @@ def tile_picked_zlayout_silu_po_kernel(
                 lhsT=w_codes[name, t].bitcast(FP8X4),
                 lhsT_scale=w_scales[name, t],
                 rhs=picked[name][:, cols].bitcast(FP8X4),
-                rhs_scale=picked_scales[name][tables[name][4] :, cols],
+                rhs_scale=picked_scales[name][FIRST_ROW[name] :, cols],
                 start=(name == "e"),
                 stop=(name == "x"),
             )
@@ -187,54 +203,48 @@ def tile_picked_zlayout_silu_po_kernel(
         out_scales = sbuf_tile([P, S], U8, "out_scales")
         out_bf16 = sbuf_tile([P, S, PACK], BF16, "out_bf16")
         out_rows = out_0.rearrange("(p t) j -> p t j", t=PACK)
-        hidden, result, h_tiles = {}, {}, {}
+        hidden, result = {}, {}
 
-        def first_product(c, direct):
+        def first_product(c):
             h_bf16 = sbuf_tile([P, CHUNK, PACK], BF16, "h_bf16_%d" % c)
-            h_pairs = None if direct else sbuf_tile([P, PAIR, CHUNK, PAIR], BF16, "h_pairs_%d" % c)
+            h_pairs = sbuf_tile([P, PAIR, CHUNK, PAIR], BF16, "h_pairs_%d" % c)
             for u in range(PAIR):
                 first_pass(c, PAIR * u, "x")
                 for name in ("e", "y", "x"):
                     first_pass(c, PAIR * u + 1, name)
-                target = h_bf16[:, :, PAIR * u : PAIR * u + PAIR] if direct else h_pairs[:, u, :, :]
-                nc.scalar.activation(target, h_banks[c, u][:].rearrange("p t n -> p n t"), SILU)
-            if not direct:
-                nc.vector.tensor_copy(
-                    h_bf16[:].rearrange("p n t -> p (n t)").bitcast(I32).rearrange("p (n u) -> p n u", u=PAIR),
-                    h_pairs[:].rearrange("p u n t -> p (u n t)").bitcast(I32).rearrange("p (u n) -> p n u", u=PAIR),
-                )
+                nc.scalar.activation(h_pairs[:, u, :, :], h_banks[c, u][:].rearrange("p t n -> p n t"), SILU)
+            nc.vector.tensor_copy(
+                h_bf16[:].rearrange("p n t -> p (n t)").bitcast(I32).rearrange("p (n u) -> p n u", u=PAIR),
+                h_pairs[:].rearrange("p u n t -> p (u n t)").bitcast(I32).rearrange("p (u n) -> p n u", u=PAIR),
+            )
             h_codes = sbuf_tile([P, CHUNK], U32, "h_codes_%d" % c)
             h_scales = sbuf_tile([P, CHUNK], U8, "h_scales_%d" % c)
             nc.vector.quantize_mx(out=h_codes[:].bitcast(FP8X4), scales=h_scales[:], in_=h_bf16[:].rearrange("p n t -> p (n t)"))
             hidden[c] = (h_codes, h_scales)
-            h_tiles[c] = h_bf16
-            h_tiles[c, 0] = h_pairs
 
-        def second_product(c, copies):
+        def second_product(c):
             cols = slice(c * CHUNK, (c + 1) * CHUNK)
             h_codes, h_scales = hidden[c]
             result[c] = sbuf_tile([P, PACK, CHUNK], F32, "result_%d" % c)
-            share = PACK // len(copies)
-            for u, copy_out in enumerate(copies):
-                bank = psum.tile([P, share, CHUNK], F32, name="out_bank_%d_%d" % (c, u), tag=bank_tag(c, u))
-                for i in range(share):
-                    m_cols = slice((u * share + i) * P, (u * share + i + 1) * P)
-                    nc.tensor.matmul_mx(
-                        out=bank[:, i, :],
-                        lhsT=w4_dealt[:, m_cols].bitcast(FP8X4),
-                        lhsT_scale=w4_dealt_scales[W4_ROW:, m_cols],
-                        rhs=h_codes[:].bitcast(FP8X4),
-                        rhs_scale=h_scales[:],
-                        start=True,
-                        stop=True,
-                    )
-                copy_out(result[c][:, u * share : (u + 1) * share, :], bank[:])
+            bank = psum.tile([P, PACK, CHUNK], F32, name="out_bank_%d" % c, tag=bank_tag(c, 0))
+            for t in range(PACK):
+                m_cols = slice(t * P, (t + 1) * P)
+                nc.tensor.matmul_mx(
+                    out=bank[:, t, :],
+                    lhsT=w4_dealt[:, m_cols].bitcast(FP8X4),
+                    lhsT_scale=w4_dealt_scales[FIRST_ROW["w4"] :, m_cols],
+                    rhs=h_codes[:].bitcast(FP8X4),
+                    rhs_scale=h_scales[:],
+                    start=True,
+                    stop=True,
+                )
+            nc.scalar.copy(result[c][:], bank[:])
             nc.sync.dma_start(out=out_rows[:, :, cols], in_=result[c][:])
 
         def round_result(c):
             nc.vector.tensor_copy(
-                out_bf16[:, c * CHUNK : (c + 1) * CHUNK, :].rearrange("p (g i) t -> p g t i", i=4),
-                result[c][:].rearrange("p t (g i) -> p g t i", i=4),
+                out_bf16[:, c * CHUNK : (c + 1) * CHUNK, :].rearrange("p (g i) t -> p g t i", i=LINE // 4),
+                result[c][:].rearrange("p t (g i) -> p g t i", i=LINE // 4),
             )
 
         def quantize_result(c0, c1):
@@ -245,24 +255,22 @@ def tile_picked_zlayout_silu_po_kernel(
             cols = slice(c0 * CHUNK, c1 * CHUNK)
             nc.sync.dma_start(out=words_view(out_1)[:, cols], in_=out_words[:, cols])
 
-        first_product(0, False)
-        first_product(1, False)
-        first_product(2, False)
-        first_product(3, False)
-        second_product(0, [nc.scalar.copy])
-        second_product(1, [nc.scalar.copy])
-        second_product(2, [nc.scalar.copy])
-        second_product(3, [nc.scalar.copy, nc.vector.tensor_copy])
-        round_result(0)
-        round_result(1)
-        quantize_result(0, 2)
-        store_words(0, 2)
-        round_result(2)
-        round_result(3)
-        quantize_result(2, 3)
-        quantize_result(3, 4)
-        store_words(2, 4)
+        for c in range(CHUNKS):
+            first_product(c)
+        for c in range(CHUNKS):
+            second_product(c)
 
-        for q in range(4):
-            queue = nc.sync if q % 2 == 0 else nc.scalar
-            queue.dma_start(out=out_2[0, q:16:4, :].bitcast(I32), in_=out_scales[q:P:32, :].bitcast(I32))
+        half = CHUNKS // 2
+        for c in range(half):
+            round_result(c)
+        quantize_result(0, half)
+        store_words(0, half)
+        for c in range(half, CHUNKS):
+            round_result(c)
+        for c in range(half, CHUNKS):
+            quantize_result(c, c + 1)
+        store_words(half, CHUNKS)
+
+        for r in range(4):
+            queue = nc.sync if r % 2 == 0 else nc.scalar
+            queue.dma_start(out=out_2[0, r:16:4, :].bitcast(I32), in_=out_scales[r:P:32, :].bitcast(I32))

@@ -24,16 +24,18 @@ LINE = 16
 ALIGN = 64
 X_PIECES = 2
 
-FIRST_ROW = {"x": 0, "e": 4, "y": 8, "w4": 12}
+FIRST_ROW = {"picked": 4, "w4": 12}
+SPREAD = P // 16
 
 PAIR_BYTES = PAIR * P * PACK * 2
-TABLE_X_AT = 0
-W4_SCALES_AT = TABLE_X_AT + 4 * N
-PLANE_X_AT = 4 * T
-W1_HIGH_AT = PLANE_X_AT + 2 * H
-W2_AT = PLANE_X_AT + H + 2 * PAIR_BYTES
-W1_LOW_AT = W2_AT + 2 * PAIR_BYTES + 4 * S
-PICKED_X_AT = W1_LOW_AT - 4 * S + ALIGN
+TABLE_Y_AT = 0
+W4_SCALES_AT = TABLE_Y_AT + 4 * N
+PLANE_W4_AT = TABLE_Y_AT + 4 * W
+W4_RAW_AT = PLANE_W4_AT + N
+PLANE_X_AT = PLANE_W4_AT - N
+TABLE_X_AT = W4_RAW_AT + 4 * N
+W3_LOW_AT = TABLE_X_AT + 4 * T + 4 * S
+PICKED_X_AT = W3_LOW_AT - 4 * S + ALIGN
 
 
 def tile_picked_zlayout_silu_po_kernel(
@@ -61,18 +63,22 @@ def tile_picked_zlayout_silu_po_kernel(
         columns = {"e": W, "x": T, "y": W}
 
         plane = {}
-        plane["x"] = sbuf_tile([P, T], U8, "plane_x", PLANE_X_AT)
-        plane["y"] = sbuf_tile([P, W], U8, "plane_y")
-        plane["e"] = sbuf_tile([P, W], U8, "plane_e")
+        for name in ("e", "y", "x"):
+            plane[name] = sbuf_tile([P, columns[name]], U8, "plane_" + name, PLANE_X_AT if name == "x" else None)
         plane["w4"] = sbuf_tile([P, N], U8, "plane_w4")
+        placed = sbuf_tile([P, 3, S], U8, "placed")
         for name in ("e", "y", "x", "w4"):
             nc.vector.memset(plane[name][:].bitcast(I32), 0)
+        nc.vector.memset(placed[:].bitcast(I32), 0)
 
         raw, lists, table = {}, {}, {}
 
         def load_scales(name):
+            nc.sync.dma_start(out=plane[name][0:P:SPREAD, :].bitcast(I32), in_=scales_in[name][0].bitcast(I32))
+
+        def load_w4_scales():
             for r in range(4):
-                nc.sync.dma_start(out=plane[name][FIRST_ROW[name] + r : P : 32, :].bitcast(I32), in_=scales_in[name][0, r:16:4, :].bitcast(I32))
+                nc.sync.dma_start(out=plane["w4"][FIRST_ROW["w4"] + r : P : 32, :].bitcast(I32), in_=w4_scales[0, r:16:4, :].bitcast(I32))
 
         def load_weight(name):
             raw[name] = sbuf_tile([P, PACK, H], F32, "raw_" + name)
@@ -87,26 +93,31 @@ def tile_picked_zlayout_silu_po_kernel(
             nc.sync.dma_start(out=table[name][:], in_=words_view(words_in[name]))
 
         load_table("e")
-        load_list("e")
-        load_list("y")
-        load_scales("e")
+        for name in ("e", "y", "x"):
+            load_list(name)
+        for name in ("e", "y", "x"):
+            load_scales(name)
         load_weight("e")
-        load_scales("y")
-        load_list("x")
-        load_table("y")
-        load_weight("y")
-        load_scales("x")
         load_weight("x")
-        load_scales("w4")
+        load_weight("y")
+        load_w4_scales()
         load_table("x", TABLE_X_AT)
-        w4_raw = sbuf_tile([P, N], I32, "w4_raw")
-        nc.sync.dma_start(out=w4_raw[:], in_=words_view(w4_words))
 
         picked_scales, picked = {}, {}
 
-        def gather_scales(name, at=None):
-            picked_scales[name] = sbuf_tile([P, S], U8, "picked_scales_" + name, at)
-            nc.vector.tensor_copy(picked_scales[name][:], plane[name][:].indirect(lists[name][:]))
+        spread = sbuf_tile([P, 3, S], U8, "spread")
+        for i, name in enumerate(("e", "y", "x")):
+            nc.vector.tensor_copy(spread[:, i, :], plane[name][:].indirect(lists[name][:]))
+            picked_scales[name] = placed[FIRST_ROW["picked"] :, i, :]
+        for r in range(4):
+            nc.sync.dma_start(
+                out=placed[FIRST_ROW["picked"] + r : P : 32, :, :].rearrange("p i n -> p (i n)").bitcast(I32),
+                in_=spread[SPREAD * r : P : 32, :, :].rearrange("p i n -> p (i n)").bitcast(I32),
+            )
+
+        load_table("y", TABLE_Y_AT)
+        w4_raw = sbuf_tile([P, N], I32, "w4_raw", W4_RAW_AT)
+        nc.sync.dma_start(out=w4_raw[:], in_=words_view(w4_words))
 
         def gather_words(name, pieces=1, at=None):
             picked[name] = sbuf_tile([P, S], U32, "picked_" + name, at)
@@ -115,7 +126,7 @@ def tile_picked_zlayout_silu_po_kernel(
                 offsets = lists[name][:, c0 // GROUP : (c0 + width) // GROUP]
                 nc.vector.tensor_copy(picked[name][:, c0 : c0 + width], table[name][:].bitcast(U32).indirect(offsets))
 
-        rounded, w_codes, w_scales = {}, {}, {}
+        rounded, w_codes, w_scales, w_planes = {}, {}, {}, {}
 
         def round_weight(name, copy, t0, t1, at=None):
             rounded[name, t0] = sbuf_tile([P, t1 - t0, P, PACK], BF16, "rounded_%s_%d" % (name, t0), at)
@@ -128,55 +139,53 @@ def tile_picked_zlayout_silu_po_kernel(
             codes = sbuf_tile([P, (t1 - t0) * P], U32, "w_codes_%s_%d" % (name, t0))
             scales = sbuf_tile([P, (t1 - t0) * P], U8, "w_scales_%s_%d" % (name, t0), at)
             nc.vector.quantize_mx(out=codes[:].bitcast(FP8X4), scales=scales[:], in_=rounded[name, t0][:].rearrange("p t m j -> p (t m j)"))
+            w_planes[name, t0] = scales
             for t in range(t0, t1):
                 w_codes[name, t] = codes[:, (t - t0) * P : (t - t0 + 1) * P]
                 w_scales[name, t] = scales[:, (t - t0) * P : (t - t0 + 1) * P]
 
         gather_words("e")
-        gather_scales("e")
-        gather_scales("y")
-        gather_words("y")
-        round_weight("e", nc.scalar.copy, 0, PACK, W2_AT)
+        round_weight("e", nc.scalar.copy, 0, PACK)
         quantize_weight("e", 0, PACK)
-        gather_scales("x", W2_AT)
-        round_weight("y", nc.scalar.copy, 0, PACK)
-        round_weight("x", nc.scalar.copy, 0, PAIR, W1_LOW_AT)
-        round_weight("x", nc.vector.tensor_copy, PAIR, PACK, W1_HIGH_AT)
-        quantize_weight("y", 0, PACK, PLANE_X_AT)
-        quantize_weight("x", PAIR, PACK)
-        quantize_weight("x", 0, PAIR)
-        gather_words("x", X_PIECES, PICKED_X_AT)
-
-        w4_dealt_scales = sbuf_tile([P, N], U8, "w4_dealt_scales", W4_SCALES_AT)
+        round_weight("x", nc.scalar.copy, 0, PACK)
+        round_weight("y", nc.scalar.copy, 0, PAIR, W3_LOW_AT)
+        round_weight("y", nc.vector.tensor_copy, PAIR, PACK)
+        quantize_weight("x", 0, PACK)
+        quantize_weight("y", PAIR, PACK)
+        w4_dealt_scales = sbuf_tile([P, N], U8, "w4_dealt_scales")
         nc.vector.tensor_copy(
             w4_dealt_scales[:].rearrange("p (t g i) -> p g t i", t=PACK, i=LINE),
             plane["w4"][:].rearrange("p (g i t) -> p g t i", t=PACK, i=LINE),
         )
-        w4_dealt = sbuf_tile([P, N], I32, "w4_dealt", TABLE_X_AT)
+        quantize_weight("y", 0, PAIR)
+        gather_words("x", X_PIECES, PICKED_X_AT)
+        gather_words("y", CHUNKS)
+
+        w4_dealt = sbuf_tile([P, N], I32, "w4_dealt", TABLE_Y_AT)
         nc.vector.tensor_copy(
             w4_dealt[:].rearrange("p (t g i) -> p g t i", t=PACK, i=LINE // 4),
             w4_raw[:].rearrange("p (g i t) -> p g t i", t=PACK, i=LINE // 4),
         )
 
+        warm_scales = w_planes["e", 0]
+
         def bank_tag(c, u):
             return "bank_%d_%d" % (c, u)
 
-        def warm_up(weight, t, scales, c, u):
-            warm = psum.tile([P, S], F32, name="warm_%d_%d" % (c, u), tag=bank_tag(c, u))
+        def warm_up(weight, t, c, u):
+            warm = psum.tile([P, S], F32, name="warm_%s_%d" % (weight, t), tag=bank_tag(c, u))
             nc.tensor.matmul_mx(
                 out=warm[:],
                 lhsT=w_codes[weight, t].bitcast(FP8X4),
                 lhsT_scale=w_scales[weight, t],
                 rhs=picked["e"][:].bitcast(FP8X4),
-                rhs_scale=picked_scales[scales][FIRST_ROW[scales] :, :],
+                rhs_scale=warm_scales[:],
                 start=True,
                 stop=True,
             )
 
-        warm_up("e", 0, "e", 1, 1)
-        warm_up("e", 1, "x", 2, 1)
-        warm_up("e", 2, "x", 3, 0)
-        warm_up("e", 3, "x", 3, 1)
+        for t in range(PACK):
+            warm_up("e", t, t, 0)
         h_banks = {}
         for c in range(CHUNKS):
             for u in range(PAIR):
@@ -189,12 +198,12 @@ def tile_picked_zlayout_silu_po_kernel(
                 lhsT=w_codes[name, t].bitcast(FP8X4),
                 lhsT_scale=w_scales[name, t],
                 rhs=picked[name][:, cols].bitcast(FP8X4),
-                rhs_scale=picked_scales[name][FIRST_ROW[name] :, cols],
+                rhs_scale=picked_scales[name][:, cols],
                 start=(name == "e"),
-                stop=(name == "x"),
+                stop=(name == "y"),
             )
 
-        for name in ("e", "y"):
+        for name in ("e", "x"):
             for c in range(CHUNKS):
                 for u in range(PAIR):
                     first_pass(c, PAIR * u, name)
@@ -209,8 +218,8 @@ def tile_picked_zlayout_silu_po_kernel(
             h_bf16 = sbuf_tile([P, CHUNK, PACK], BF16, "h_bf16_%d" % c)
             h_pairs = sbuf_tile([P, PAIR, CHUNK, PAIR], BF16, "h_pairs_%d" % c)
             for u in range(PAIR):
-                first_pass(c, PAIR * u, "x")
-                for name in ("e", "y", "x"):
+                first_pass(c, PAIR * u, "y")
+                for name in ("e", "x", "y"):
                     first_pass(c, PAIR * u + 1, name)
                 nc.scalar.activation(h_pairs[:, u, :, :], h_banks[c, u][:].rearrange("p t n -> p n t"), SILU)
             nc.vector.tensor_copy(

@@ -126,7 +126,7 @@ def tile_picked_zlayout_silu_po_kernel(
                 offsets = lists[name][:, c0 // GROUP : (c0 + width) // GROUP]
                 nc.vector.tensor_copy(picked[name][:, c0 : c0 + width], table[name][:].bitcast(U32).indirect(offsets))
 
-        rounded, w_codes, w_scales, w_planes = {}, {}, {}, {}
+        rounded, w_codes, w_scales = {}, {}, {}
 
         def round_weight(name, copy, t0, t1, at=None):
             rounded[name, t0] = sbuf_tile([P, t1 - t0, P, PACK], BF16, "rounded_%s_%d" % (name, t0), at)
@@ -139,7 +139,6 @@ def tile_picked_zlayout_silu_po_kernel(
             codes = sbuf_tile([P, (t1 - t0) * P], U32, "w_codes_%s_%d" % (name, t0))
             scales = sbuf_tile([P, (t1 - t0) * P], U8, "w_scales_%s_%d" % (name, t0), at)
             nc.vector.quantize_mx(out=codes[:].bitcast(FP8X4), scales=scales[:], in_=rounded[name, t0][:].rearrange("p t m j -> p (t m j)"))
-            w_planes[name, t0] = scales
             for t in range(t0, t1):
                 w_codes[name, t] = codes[:, (t - t0) * P : (t - t0 + 1) * P]
                 w_scales[name, t] = scales[:, (t - t0) * P : (t - t0 + 1) * P]
@@ -167,8 +166,6 @@ def tile_picked_zlayout_silu_po_kernel(
             w4_raw[:].rearrange("p (g i t) -> p g t i", t=PACK, i=LINE // 4),
         )
 
-        warm_scales = w_planes["e", 0]
-
         def bank_tag(c, u):
             return "bank_%d_%d" % (c, u)
 
@@ -179,7 +176,7 @@ def tile_picked_zlayout_silu_po_kernel(
                 lhsT=w_codes[weight, t].bitcast(FP8X4),
                 lhsT_scale=w_scales[weight, t],
                 rhs=picked["e"][:].bitcast(FP8X4),
-                rhs_scale=warm_scales[:],
+                rhs_scale=plane["w4"][FIRST_ROW["w4"] :, :],
                 start=True,
                 stop=True,
             )

@@ -183,27 +183,27 @@ def tile_picked_zlayout_silu_po_kernel(
 
         for t in range(PACK):
             warm_up("e", t, t, 0)
-        h_banks = {}
-        for c in range(CHUNKS):
-            for u in range(PAIR):
-                h_banks[c, u] = psum.tile([P, PAIR, CHUNK], F32, name="h_bank_%d_%d" % (c, u), tag=bank_tag(c, u))
+        h_banks = [psum.tile([P, PACK, CHUNK], F32, name="h_bank_%d" % c, tag=bank_tag(c, 1)) for c in range(CHUNKS)]
 
-        def first_pass(c, t, name):
+        order = [["e", "x", "y"], ["e", "x", "y"], ["e", "y", "x"], ["y", "e", "x"]]
+
+        def first_passes(c, name):
             cols = slice(c * CHUNK, (c + 1) * CHUNK)
-            nc.tensor.matmul_mx(
-                out=h_banks[c, t // PAIR][:, t % PAIR, :],
-                lhsT=w_codes[name, t].bitcast(FP8X4),
-                lhsT_scale=w_scales[name, t],
-                rhs=picked[name][:, cols].bitcast(FP8X4),
-                rhs_scale=picked_scales[name][:, cols],
-                start=(name == "e"),
-                stop=(name == "y"),
-            )
+            for t in range(PACK):
+                nc.tensor.matmul_mx(
+                    out=h_banks[c][:, t, :],
+                    lhsT=w_codes[name, t].bitcast(FP8X4),
+                    lhsT_scale=w_scales[name, t],
+                    rhs=picked[name][:, cols].bitcast(FP8X4),
+                    rhs_scale=picked_scales[name][:, cols],
+                    start=(name == order[c][0] and t == 0),
+                    stop=(name == order[c][-1] and t == PACK - 1),
+                )
 
         for name in ("e", "x"):
             for c in range(CHUNKS):
-                for u in range(PAIR):
-                    first_pass(c, PAIR * u, name)
+                if name in order[c][: order[c].index("y")]:
+                    first_passes(c, name)
 
         out_words = sbuf_tile([P, S], I32, "out_words")
         out_scales = sbuf_tile([P, S], U8, "out_scales")
@@ -213,16 +213,9 @@ def tile_picked_zlayout_silu_po_kernel(
 
         def first_product(c):
             h_bf16 = sbuf_tile([P, CHUNK, PACK], BF16, "h_bf16_%d" % c)
-            h_pairs = sbuf_tile([P, PAIR, CHUNK, PAIR], BF16, "h_pairs_%d" % c)
-            for u in range(PAIR):
-                first_pass(c, PAIR * u, "y")
-                for name in ("e", "x", "y"):
-                    first_pass(c, PAIR * u + 1, name)
-                nc.scalar.activation(h_pairs[:, u, :, :], h_banks[c, u][:].rearrange("p t n -> p n t"), SILU)
-            nc.vector.tensor_copy(
-                h_bf16[:].rearrange("p n t -> p (n t)").bitcast(I32).rearrange("p (n u) -> p n u", u=PAIR),
-                h_pairs[:].rearrange("p u n t -> p (u n t)").bitcast(I32).rearrange("p (u n) -> p n u", u=PAIR),
-            )
+            for name in order[c][order[c].index("y") :]:
+                first_passes(c, name)
+            nc.scalar.activation(h_bf16[:], h_banks[c][:].rearrange("p t n -> p n t"), SILU)
             h_codes = sbuf_tile([P, CHUNK], U32, "h_codes_%d" % c)
             h_scales = sbuf_tile([P, CHUNK], U8, "h_scales_%d" % c)
             nc.vector.quantize_mx(out=h_codes[:].bitcast(FP8X4), scales=h_scales[:], in_=h_bf16[:].rearrange("p n t -> p (n t)"))
@@ -244,7 +237,8 @@ def tile_picked_zlayout_silu_po_kernel(
                     start=True,
                     stop=True,
                 )
-            nc.scalar.copy(result[c][:], bank[:])
+            copy = nc.vector.tensor_copy if c == 0 else nc.scalar.copy
+            copy(result[c][:], bank[:])
             nc.sync.dma_start(out=out_rows[:, :, cols], in_=result[c][:])
 
         def round_result(c):
@@ -270,12 +264,10 @@ def tile_picked_zlayout_silu_po_kernel(
         for c in range(half):
             round_result(c)
         quantize_result(0, half)
-        store_words(0, half)
         for c in range(half, CHUNKS):
             round_result(c)
-        for c in range(half, CHUNKS):
             quantize_result(c, c + 1)
-        store_words(half, CHUNKS)
+        store_words(0, CHUNKS)
 
         for r in range(4):
             queue = nc.sync if r % 2 == 0 else nc.scalar

@@ -24,7 +24,7 @@ LINE = 16
 ALIGN = 64
 X_PIECES = 2
 
-FIRST_ROW = {"picked": 4, "w4": 12}
+FIRST_ROW = {"placed": 4, "e": 8, "w4": 12}
 SPREAD = P // 16
 
 PAIR_BYTES = PAIR * P * PACK * 2
@@ -66,7 +66,7 @@ def tile_picked_zlayout_silu_po_kernel(
         for name in ("e", "y", "x"):
             plane[name] = sbuf_tile([P, columns[name]], U8, "plane_" + name, PLANE_X_AT if name == "x" else None)
         plane["w4"] = sbuf_tile([P, N], U8, "plane_w4")
-        placed = sbuf_tile([P, 3, S], U8, "placed")
+        placed = sbuf_tile([P, 2, S], U8, "placed")
         for name in ("e", "y", "x", "w4"):
             nc.vector.memset(plane[name][:].bitcast(I32), 0)
         nc.vector.memset(placed[:].bitcast(I32), 0)
@@ -76,9 +76,9 @@ def tile_picked_zlayout_silu_po_kernel(
         def load_scales(name):
             nc.sync.dma_start(out=plane[name][0:P:SPREAD, :].bitcast(I32), in_=scales_in[name][0].bitcast(I32))
 
-        def load_w4_scales():
+        def load_scales_in_place(name):
             for r in range(4):
-                nc.sync.dma_start(out=plane["w4"][FIRST_ROW["w4"] + r : P : 32, :].bitcast(I32), in_=w4_scales[0, r:16:4, :].bitcast(I32))
+                nc.sync.dma_start(out=plane[name][FIRST_ROW[name] + r : P : 32, :].bitcast(I32), in_=scales_in[name][0, r:16:4, :].bitcast(I32))
 
         def load_weight(name):
             raw[name] = sbuf_tile([P, PACK, H], F32, "raw_" + name)
@@ -93,25 +93,30 @@ def tile_picked_zlayout_silu_po_kernel(
             nc.sync.dma_start(out=table[name][:], in_=words_view(words_in[name]))
 
         load_table("e")
-        for name in ("e", "y", "x"):
-            load_list(name)
-        for name in ("e", "y", "x"):
-            load_scales(name)
+        load_list("e")
+        load_list("y")
+        load_scales_in_place("e")
         load_weight("e")
+        load_list("x")
+        load_scales("y")
+        load_scales("x")
         load_weight("x")
         load_weight("y")
-        load_w4_scales()
+        load_scales_in_place("w4")
         load_table("x", TABLE_X_AT)
 
         picked_scales, picked = {}, {}
 
-        spread = sbuf_tile([P, 3, S], U8, "spread")
-        for i, name in enumerate(("e", "y", "x")):
+        spread = sbuf_tile([P, 2, S], U8, "spread")
+        e_picked = sbuf_tile([P, S], U8, "picked_scales_e")
+        nc.vector.tensor_copy(e_picked[:], plane["e"][:].indirect(lists["e"][:]))
+        picked_scales["e"] = e_picked[FIRST_ROW["e"] :, :]
+        for i, name in enumerate(("y", "x")):
             nc.vector.tensor_copy(spread[:, i, :], plane[name][:].indirect(lists[name][:]))
-            picked_scales[name] = placed[FIRST_ROW["picked"] :, i, :]
+            picked_scales[name] = placed[FIRST_ROW["placed"] :, i, :]
         for r in range(4):
             nc.sync.dma_start(
-                out=placed[FIRST_ROW["picked"] + r : P : 32, :, :].rearrange("p i n -> p (i n)").bitcast(I32),
+                out=placed[FIRST_ROW["placed"] + r : P : 32, :, :].rearrange("p i n -> p (i n)").bitcast(I32),
                 in_=spread[SPREAD * r : P : 32, :, :].rearrange("p i n -> p (i n)").bitcast(I32),
             )
 
@@ -146,16 +151,18 @@ def tile_picked_zlayout_silu_po_kernel(
         gather_words("e")
         round_weight("e", nc.scalar.copy, 0, PACK)
         quantize_weight("e", 0, PACK)
-        round_weight("x", nc.scalar.copy, 0, PACK)
+        round_weight("x", nc.scalar.copy, 0, PAIR)
+        round_weight("x", nc.vector.tensor_copy, PAIR, PACK)
+        quantize_weight("x", 0, PAIR)
+        quantize_weight("x", PAIR, PACK)
         round_weight("y", nc.scalar.copy, 0, PAIR, W3_LOW_AT)
         round_weight("y", nc.vector.tensor_copy, PAIR, PACK)
-        quantize_weight("x", 0, PACK)
-        quantize_weight("y", PAIR, PACK)
         w4_dealt_scales = sbuf_tile([P, N], U8, "w4_dealt_scales")
         nc.vector.tensor_copy(
             w4_dealt_scales[:].rearrange("p (t g i) -> p g t i", t=PACK, i=LINE),
             plane["w4"][:].rearrange("p (g i t) -> p g t i", t=PACK, i=LINE),
         )
+        quantize_weight("y", PAIR, PACK)
         quantize_weight("y", 0, PAIR)
         gather_words("x", X_PIECES, PICKED_X_AT)
         gather_words("y", CHUNKS)
@@ -185,7 +192,7 @@ def tile_picked_zlayout_silu_po_kernel(
             warm_up("e", t, t, 0)
         h_banks = [psum.tile([P, PACK, CHUNK], F32, name="h_bank_%d" % c, tag=bank_tag(c, 1)) for c in range(CHUNKS)]
 
-        order = [["e", "x", "y"], ["e", "x", "y"], ["e", "y", "x"], ["y", "e", "x"]]
+        order = [["e", "x", "y"]] * (CHUNKS - 1) + [["e", "y", "x"]]
 
         def first_passes(c, name):
             cols = slice(c * CHUNK, (c + 1) * CHUNK)
@@ -264,10 +271,11 @@ def tile_picked_zlayout_silu_po_kernel(
         for c in range(half):
             round_result(c)
         quantize_result(0, half)
+        store_words(0, half)
         for c in range(half, CHUNKS):
             round_result(c)
             quantize_result(c, c + 1)
-        store_words(0, CHUNKS)
+        store_words(half, CHUNKS)
 
         for r in range(4):
             queue = nc.sync if r % 2 == 0 else nc.scalar

@@ -96,11 +96,11 @@ def tile_picked_zlayout_silu_po_kernel(
         load_list("e")
         load_list("y")
         load_scales_in_place("e")
-        load_weight("e")
+        load_weight("x")
         load_list("x")
         load_scales("y")
         load_scales("x")
-        load_weight("x")
+        load_weight("e")
         load_weight("y")
         load_scales_in_place("w4")
         load_table("x", TABLE_X_AT)
@@ -149,12 +149,12 @@ def tile_picked_zlayout_silu_po_kernel(
                 w_scales[name, t] = scales[:, (t - t0) * P : (t - t0 + 1) * P]
 
         gather_words("e")
-        round_weight("e", nc.scalar.copy, 0, PACK)
-        quantize_weight("e", 0, PACK)
-        round_weight("x", nc.scalar.copy, 0, PAIR)
-        round_weight("x", nc.vector.tensor_copy, PAIR, PACK)
-        quantize_weight("x", 0, PAIR)
-        quantize_weight("x", PAIR, PACK)
+        round_weight("x", nc.scalar.copy, 0, PACK)
+        quantize_weight("x", 0, PACK)
+        round_weight("e", nc.scalar.copy, 0, PAIR)
+        round_weight("e", nc.vector.tensor_copy, PAIR, PACK)
+        quantize_weight("e", 0, PAIR)
+        quantize_weight("e", PAIR, PACK)
         round_weight("y", nc.scalar.copy, 0, PAIR, W3_LOW_AT)
         round_weight("y", nc.vector.tensor_copy, PAIR, PACK)
         w4_dealt_scales = sbuf_tile([P, N], U8, "w4_dealt_scales")
@@ -176,20 +176,6 @@ def tile_picked_zlayout_silu_po_kernel(
         def bank_tag(c, u):
             return "bank_%d_%d" % (c, u)
 
-        def warm_up(weight, t, c, u):
-            warm = psum.tile([P, S], F32, name="warm_%s_%d" % (weight, t), tag=bank_tag(c, u))
-            nc.tensor.matmul_mx(
-                out=warm[:],
-                lhsT=w_codes[weight, t].bitcast(FP8X4),
-                lhsT_scale=w_scales[weight, t],
-                rhs=picked["e"][:].bitcast(FP8X4),
-                rhs_scale=plane["w4"][FIRST_ROW["w4"] :, :],
-                start=True,
-                stop=True,
-            )
-
-        for t in range(PACK):
-            warm_up("e", t, t, 0)
         h_banks = [psum.tile([P, PACK, CHUNK], F32, name="h_bank_%d" % c, tag=bank_tag(c, 1)) for c in range(CHUNKS)]
 
         order = [["e", "x", "y"]] * (CHUNKS - 1) + [["e", "y", "x"]]

@@ -21,7 +21,7 @@ CHUNK = 128
 CHUNKS = S // CHUNK
 GROUP = 16
 LINE = 16
-ALIGN = 64
+ALIGN = 256
 X_PIECES = 2
 
 FIRST_ROW = {"placed": 4, "e": 8, "w4": 12}

@@ -23,19 +23,18 @@ GROUP = 16
 LINE = 16
 ALIGN = 256
 X_PIECES = 2
+ROWS = 16
+SPREAD = P // ROWS
+TABLES_FIRST = 4
+W4_FIRST = 12
 
-FIRST_ROW = {"placed": 4, "e": 8, "w4": 12}
-SPREAD = P // 16
-
-PAIR_BYTES = PAIR * P * PACK * 2
-TABLE_Y_AT = 0
-W4_SCALES_AT = TABLE_Y_AT + 4 * N
-PLANE_W4_AT = TABLE_Y_AT + 4 * W
-W4_RAW_AT = PLANE_W4_AT + N
-PLANE_X_AT = PLANE_W4_AT - N
-TABLE_X_AT = W4_RAW_AT + 4 * N
-W3_LOW_AT = TABLE_X_AT + 4 * T + 4 * S
-PICKED_X_AT = W3_LOW_AT - 4 * S + ALIGN
+TABLE_X_AT = 0
+PLANE_E_AT = TABLE_X_AT + 4 * T - ALIGN
+TABLE_Y_AT = PLANE_E_AT + W - ALIGN
+RAW_E_AT = TABLE_Y_AT + 4 * W
+PICKED_X_AT = RAW_E_AT + 4 * PACK * H
+W3_LOW_AT = PICKED_X_AT + 4 * S - ALIGN
+H_CODES_AT = W3_LOW_AT + PAIR * P * PACK * 2
 
 
 def tile_picked_zlayout_silu_po_kernel(
@@ -60,28 +59,26 @@ def tile_picked_zlayout_silu_po_kernel(
         scales_in = {"e": e_scales, "x": x_scales, "y": y_scales, "w4": w4_scales}
         list_in = {"e": tok, "x": offs, "y": row}
         weight_in = {"e": w2, "x": w1, "y": w3}
-        columns = {"e": W, "x": T, "y": W}
+        columns = {"e": W, "x": T, "y": W, "w4": N}
+        tables = ("y", "x", "e")
 
+        plane_at = {"e": PLANE_E_AT}
         plane = {}
-        for name in ("e", "y", "x"):
-            plane[name] = sbuf_tile([P, columns[name]], U8, "plane_" + name, PLANE_X_AT if name == "x" else None)
-        plane["w4"] = sbuf_tile([P, N], U8, "plane_w4")
-        placed = sbuf_tile([P, 2, S], U8, "placed")
-        for name in ("e", "y", "x", "w4"):
+        for name in tables + ("w4",):
+            plane[name] = sbuf_tile([P, columns[name]], U8, "plane_" + name, plane_at.get(name))
             nc.vector.memset(plane[name][:].bitcast(I32), 0)
+        placed = sbuf_tile([P, len(tables), S], U8, "placed")
         nc.vector.memset(placed[:].bitcast(I32), 0)
+        w4_placed = sbuf_tile([P, N], U8, "w4_placed")
+        nc.vector.memset(w4_placed[:].bitcast(I32), 0)
 
         raw, lists, table = {}, {}, {}
 
         def load_scales(name):
             nc.sync.dma_start(out=plane[name][0:P:SPREAD, :].bitcast(I32), in_=scales_in[name][0].bitcast(I32))
 
-        def load_scales_in_place(name):
-            for r in range(4):
-                nc.sync.dma_start(out=plane[name][FIRST_ROW[name] + r : P : 32, :].bitcast(I32), in_=scales_in[name][0, r:16:4, :].bitcast(I32))
-
-        def load_weight(name):
-            raw[name] = sbuf_tile([P, PACK, H], F32, "raw_" + name)
+        def load_weight(name, at=None):
+            raw[name] = sbuf_tile([P, PACK, H], F32, "raw_" + name, at)
             nc.sync.dma_start(out=raw[name][:], in_=weight_in[name].rearrange("(p j) c -> p j c", j=PACK))
 
         def load_list(name):
@@ -92,37 +89,33 @@ def tile_picked_zlayout_silu_po_kernel(
             table[name] = sbuf_tile([P, columns[name]], I32, "table_" + name, at)
             nc.sync.dma_start(out=table[name][:], in_=words_view(words_in[name]))
 
+        def place(target, first, source):
+            for r in range(4):
+                nc.sync.dma_start(out=target[first + r : P : 32, :].bitcast(I32), in_=source[SPREAD * r : P : 32, :].bitcast(I32))
+
         load_table("e")
+        for name in ("y", "x"):
+            load_list(name)
+            load_scales(name)
+        load_weight("e", RAW_E_AT)
+        load_scales("e")
         load_list("e")
-        load_list("y")
-        load_scales_in_place("e")
         load_weight("x")
-        load_list("x")
-        load_scales("y")
-        load_scales("x")
-        load_weight("e")
+        load_scales("w4")
         load_weight("y")
-        load_scales_in_place("w4")
-        load_table("x", TABLE_X_AT)
 
-        picked_scales, picked = {}, {}
-
-        spread = sbuf_tile([P, 2, S], U8, "spread")
-        e_picked = sbuf_tile([P, S], U8, "picked_scales_e")
-        nc.vector.tensor_copy(e_picked[:], plane["e"][:].indirect(lists["e"][:]))
-        picked_scales["e"] = e_picked[FIRST_ROW["e"] :, :]
-        for i, name in enumerate(("y", "x")):
+        spread = sbuf_tile([P, len(tables), S], U8, "spread")
+        picked_scales = {}
+        for i, name in enumerate(tables):
             nc.vector.tensor_copy(spread[:, i, :], plane[name][:].indirect(lists[name][:]))
-            picked_scales[name] = placed[FIRST_ROW["placed"] :, i, :]
-        for r in range(4):
-            nc.sync.dma_start(
-                out=placed[FIRST_ROW["placed"] + r : P : 32, :, :].rearrange("p i n -> p (i n)").bitcast(I32),
-                in_=spread[SPREAD * r : P : 32, :, :].rearrange("p i n -> p (i n)").bitcast(I32),
-            )
+            picked_scales[name] = placed[TABLES_FIRST:, i, :]
+        place(placed[:].rearrange("p i n -> p (i n)"), TABLES_FIRST, spread[:].rearrange("p i n -> p (i n)"))
 
+        load_table("x", TABLE_X_AT)
         load_table("y", TABLE_Y_AT)
-        w4_raw = sbuf_tile([P, N], I32, "w4_raw", W4_RAW_AT)
-        nc.sync.dma_start(out=w4_raw[:], in_=words_view(w4_words))
+        w4_raw = sbuf_tile([P, N], I32, "w4_raw", RAW_E_AT)
+
+        picked = {}
 
         def gather_words(name, pieces=1, at=None):
             picked[name] = sbuf_tile([P, S], U32, "picked_" + name, at)
@@ -140,44 +133,42 @@ def tile_picked_zlayout_silu_po_kernel(
                 raw[name][:].rearrange("p j (m t) -> p m j t", t=PACK)[:, :, :, t0:t1],
             )
 
-        def quantize_weight(name, t0, t1, at=None):
+        def quantize_weight(name, t0, t1):
             codes = sbuf_tile([P, (t1 - t0) * P], U32, "w_codes_%s_%d" % (name, t0))
-            scales = sbuf_tile([P, (t1 - t0) * P], U8, "w_scales_%s_%d" % (name, t0), at)
+            scales = sbuf_tile([P, (t1 - t0) * P], U8, "w_scales_%s_%d" % (name, t0))
             nc.vector.quantize_mx(out=codes[:].bitcast(FP8X4), scales=scales[:], in_=rounded[name, t0][:].rearrange("p t m j -> p (t m j)"))
             for t in range(t0, t1):
                 w_codes[name, t] = codes[:, (t - t0) * P : (t - t0 + 1) * P]
                 w_scales[name, t] = scales[:, (t - t0) * P : (t - t0 + 1) * P]
 
         gather_words("e")
-        round_weight("x", nc.scalar.copy, 0, PACK)
-        quantize_weight("x", 0, PACK)
-        round_weight("e", nc.scalar.copy, 0, PAIR)
-        round_weight("e", nc.vector.tensor_copy, PAIR, PACK)
-        quantize_weight("e", 0, PAIR)
-        quantize_weight("e", PAIR, PACK)
-        round_weight("y", nc.scalar.copy, 0, PAIR, W3_LOW_AT)
-        round_weight("y", nc.vector.tensor_copy, PAIR, PACK)
-        w4_dealt_scales = sbuf_tile([P, N], U8, "w4_dealt_scales")
+        round_weight("e", nc.scalar.copy, 0, PACK)
+        nc.sync.dma_start(out=w4_raw[:], in_=words_view(w4_words))
+        quantize_weight("e", 0, PACK)
+        round_weight("x", nc.scalar.copy, 0, PAIR)
+        round_weight("x", nc.vector.tensor_copy, PAIR, PACK)
+        quantize_weight("x", PAIR, PACK)
+        quantize_weight("x", 0, PAIR)
+        w4_spread = sbuf_tile([P, N], U8, "w4_spread")
         nc.vector.tensor_copy(
-            w4_dealt_scales[:].rearrange("p (t g i) -> p g t i", t=PACK, i=LINE),
+            w4_spread[:].rearrange("p (t g i) -> p g t i", t=PACK, i=LINE),
             plane["w4"][:].rearrange("p (g i t) -> p g t i", t=PACK, i=LINE),
         )
+        place(w4_placed[:], W4_FIRST, w4_spread[:])
+        round_weight("y", nc.scalar.copy, 0, PAIR, W3_LOW_AT)
+        round_weight("y", nc.vector.tensor_copy, PAIR, PACK)
         quantize_weight("y", PAIR, PACK)
         quantize_weight("y", 0, PAIR)
         gather_words("x", X_PIECES, PICKED_X_AT)
         gather_words("y", CHUNKS)
 
-        w4_dealt = sbuf_tile([P, N], I32, "w4_dealt", TABLE_Y_AT)
+        w4_dealt = sbuf_tile([P, N], I32, "w4_dealt", TABLE_Y_AT + 4 * N)
         nc.vector.tensor_copy(
             w4_dealt[:].rearrange("p (t g i) -> p g t i", t=PACK, i=LINE // 4),
             w4_raw[:].rearrange("p (g i t) -> p g t i", t=PACK, i=LINE // 4),
         )
 
-        def bank_tag(c, u):
-            return "bank_%d_%d" % (c, u)
-
-        h_banks = [psum.tile([P, PACK, CHUNK], F32, name="h_bank_%d" % c, tag=bank_tag(c, 1)) for c in range(CHUNKS)]
-
+        h_banks = [psum.tile([P, PACK, CHUNK], F32, name="h_bank_%d" % c) for c in range(CHUNKS)]
         order = [["e", "x", "y"]] * (CHUNKS - 1) + [["e", "y", "x"]]
 
         def first_passes(c, name):
@@ -204,12 +195,18 @@ def tile_picked_zlayout_silu_po_kernel(
         out_rows = out_0.rearrange("(p t) j -> p t j", t=PACK)
         hidden, result = {}, {}
 
+        activated = {}
+
         def first_product(c):
             h_bf16 = sbuf_tile([P, CHUNK, PACK], BF16, "h_bf16_%d" % c)
             for name in order[c][order[c].index("y") :]:
                 first_passes(c, name)
             nc.scalar.activation(h_bf16[:], h_banks[c][:].rearrange("p t n -> p n t"), SILU)
-            h_codes = sbuf_tile([P, CHUNK], U32, "h_codes_%d" % c)
+            activated[c] = h_bf16
+
+        def quantize_hidden(c):
+            h_bf16 = activated[c]
+            h_codes = sbuf_tile([P, CHUNK], U32, "h_codes_%d" % c, H_CODES_AT + (c % 2) * 4 * CHUNK)
             h_scales = sbuf_tile([P, CHUNK], U8, "h_scales_%d" % c)
             nc.vector.quantize_mx(out=h_codes[:].bitcast(FP8X4), scales=h_scales[:], in_=h_bf16[:].rearrange("p n t -> p (n t)"))
             hidden[c] = (h_codes, h_scales)
@@ -218,13 +215,13 @@ def tile_picked_zlayout_silu_po_kernel(
             cols = slice(c * CHUNK, (c + 1) * CHUNK)
             h_codes, h_scales = hidden[c]
             result[c] = sbuf_tile([P, PACK, CHUNK], F32, "result_%d" % c)
-            bank = psum.tile([P, PACK, CHUNK], F32, name="out_bank_%d" % c, tag=bank_tag(c, 0))
+            bank = psum.tile([P, PACK, CHUNK], F32, name="out_bank_%d" % c)
             for t in range(PACK):
                 m_cols = slice(t * P, (t + 1) * P)
                 nc.tensor.matmul_mx(
                     out=bank[:, t, :],
                     lhsT=w4_dealt[:, m_cols].bitcast(FP8X4),
-                    lhsT_scale=w4_dealt_scales[FIRST_ROW["w4"] :, m_cols],
+                    lhsT_scale=w4_placed[W4_FIRST:, m_cols],
                     rhs=h_codes[:].bitcast(FP8X4),
                     rhs_scale=h_scales[:],
                     start=True,
@@ -250,17 +247,21 @@ def tile_picked_zlayout_silu_po_kernel(
 
         for c in range(CHUNKS):
             first_product(c)
+        quantize_hidden(0)
         for c in range(CHUNKS):
+            if c + 1 < CHUNKS:
+                quantize_hidden(c + 1)
             second_product(c)
 
         half = CHUNKS // 2
         for c in range(half):
             round_result(c)
-        quantize_result(0, half)
+        for c in range(half):
+            quantize_result(c, c + 1)
         store_words(0, half)
         for c in range(half, CHUNKS):
             round_result(c)
-            quantize_result(c, c + 1)
+        quantize_result(half, CHUNKS)
         store_words(half, CHUNKS)
 
         for r in range(4):

@@ -22,19 +22,13 @@ CHUNKS = S // CHUNK
 GROUP = 16
 LINE = 16
 ALIGN = 256
-X_PIECES = 2
 ROWS = 16
 SPREAD = P // ROWS
 TABLES_FIRST = 4
+E_FIRST = 8
 W4_FIRST = 12
 
-TABLE_X_AT = 0
-PLANE_E_AT = TABLE_X_AT + 4 * T - ALIGN
-TABLE_Y_AT = PLANE_E_AT + W - ALIGN
-RAW_E_AT = TABLE_Y_AT + 4 * W
-PICKED_X_AT = RAW_E_AT + 4 * PACK * H
-W3_LOW_AT = PICKED_X_AT + 4 * S - ALIGN
-H_CODES_AT = W3_LOW_AT + PAIR * P * PACK * 2
+H_CODES_AT = 0
 
 
 def tile_picked_zlayout_silu_po_kernel(
@@ -60,12 +54,11 @@ def tile_picked_zlayout_silu_po_kernel(
         list_in = {"e": tok, "x": offs, "y": row}
         weight_in = {"e": w2, "x": w1, "y": w3}
         columns = {"e": W, "x": T, "y": W, "w4": N}
-        tables = ("y", "x", "e")
+        tables = ("y", "x")
 
-        plane_at = {"e": PLANE_E_AT}
         plane = {}
-        for name in tables + ("w4",):
-            plane[name] = sbuf_tile([P, columns[name]], U8, "plane_" + name, plane_at.get(name))
+        for name in ("e",) + tables + ("w4",):
+            plane[name] = sbuf_tile([P, columns[name]], U8, "plane_" + name)
             nc.vector.memset(plane[name][:].bitcast(I32), 0)
         placed = sbuf_tile([P, len(tables), S], U8, "placed")
         nc.vector.memset(placed[:].bitcast(I32), 0)
@@ -93,27 +86,19 @@ def tile_picked_zlayout_silu_po_kernel(
             for r in range(4):
                 nc.sync.dma_start(out=target[first + r : P : 32, :].bitcast(I32), in_=source[SPREAD * r : P : 32, :].bitcast(I32))
 
-        load_table("e")
-        for name in ("y", "x"):
-            load_list(name)
-            load_scales(name)
-        load_weight("e", RAW_E_AT)
-        load_scales("e")
+        load_table("y")
         load_list("e")
-        load_weight("x")
-        load_scales("w4")
+        load_list("y")
+        for r in range(4):
+            nc.sync.dma_start(out=plane["e"][E_FIRST + r : P : 32, :].bitcast(I32), in_=e_scales[0, r:ROWS:4, :].bitcast(I32))
+        load_weight("e")
+        load_list("x")
+        load_scales("y")
+        load_scales("x")
         load_weight("y")
-
-        spread = sbuf_tile([P, len(tables), S], U8, "spread")
-        picked_scales = {}
-        for i, name in enumerate(tables):
-            nc.vector.tensor_copy(spread[:, i, :], plane[name][:].indirect(lists[name][:]))
-            picked_scales[name] = placed[TABLES_FIRST:, i, :]
-        place(placed[:].rearrange("p i n -> p (i n)"), TABLES_FIRST, spread[:].rearrange("p i n -> p (i n)"))
-
-        load_table("x", TABLE_X_AT)
-        load_table("y", TABLE_Y_AT)
-        w4_raw = sbuf_tile([P, N], I32, "w4_raw", RAW_E_AT)
+        load_scales("w4")
+        load_table("e")
+        load_weight("x")
 
         picked = {}
 
@@ -123,6 +108,21 @@ def tile_picked_zlayout_silu_po_kernel(
             for c0 in range(0, S, width):
                 offsets = lists[name][:, c0 // GROUP : (c0 + width) // GROUP]
                 nc.vector.tensor_copy(picked[name][:, c0 : c0 + width], table[name][:].bitcast(U32).indirect(offsets))
+
+        picked_scales = {}
+        e_picked = sbuf_tile([P, S], U8, "picked_scales_e")
+        nc.vector.tensor_copy(e_picked[:], plane["e"][:].indirect(lists["e"][:]))
+        picked_scales["e"] = e_picked[E_FIRST:, :]
+        gather_words("y")
+        spread = sbuf_tile([P, len(tables), S], U8, "spread")
+        for i, name in enumerate(tables):
+            nc.vector.tensor_copy(spread[:, i, :], plane[name][:].indirect(lists[name][:]))
+            picked_scales[name] = placed[TABLES_FIRST:, i, :]
+        place(placed[:].rearrange("p i n -> p (i n)"), TABLES_FIRST, spread[:].rearrange("p i n -> p (i n)"))
+
+        load_table("x")
+        w4_raw = sbuf_tile([P, N], I32, "w4_raw")
+        nc.sync.dma_start(out=w4_raw[:], in_=words_view(w4_words))
 
         rounded, w_codes, w_scales = {}, {}, {}
 
@@ -141,35 +141,31 @@ def tile_picked_zlayout_silu_po_kernel(
                 w_codes[name, t] = codes[:, (t - t0) * P : (t - t0 + 1) * P]
                 w_scales[name, t] = scales[:, (t - t0) * P : (t - t0 + 1) * P]
 
-        gather_words("e")
         round_weight("e", nc.scalar.copy, 0, PACK)
-        nc.sync.dma_start(out=w4_raw[:], in_=words_view(w4_words))
         quantize_weight("e", 0, PACK)
-        round_weight("x", nc.scalar.copy, 0, PAIR)
-        round_weight("x", nc.vector.tensor_copy, PAIR, PACK)
-        quantize_weight("x", PAIR, PACK)
-        quantize_weight("x", 0, PAIR)
+        round_weight("y", nc.scalar.copy, 0, PACK)
         w4_spread = sbuf_tile([P, N], U8, "w4_spread")
         nc.vector.tensor_copy(
             w4_spread[:].rearrange("p (t g i) -> p g t i", t=PACK, i=LINE),
             plane["w4"][:].rearrange("p (g i t) -> p g t i", t=PACK, i=LINE),
         )
         place(w4_placed[:], W4_FIRST, w4_spread[:])
-        round_weight("y", nc.scalar.copy, 0, PAIR, W3_LOW_AT)
-        round_weight("y", nc.vector.tensor_copy, PAIR, PACK)
-        quantize_weight("y", PAIR, PACK)
-        quantize_weight("y", 0, PAIR)
-        gather_words("x", X_PIECES, PICKED_X_AT)
-        gather_words("y", CHUNKS)
+        gather_words("e", CHUNKS)
+        quantize_weight("y", 0, PACK)
+        round_weight("x", nc.scalar.copy, 0, PAIR)
+        round_weight("x", nc.vector.tensor_copy, PAIR, PACK)
+        quantize_weight("x", PAIR, PACK)
+        quantize_weight("x", 0, PAIR)
+        gather_words("x", CHUNKS)
 
-        w4_dealt = sbuf_tile([P, N], I32, "w4_dealt", TABLE_Y_AT + 4 * N)
+        w4_dealt = sbuf_tile([P, N], I32, "w4_dealt")
         nc.vector.tensor_copy(
             w4_dealt[:].rearrange("p (t g i) -> p g t i", t=PACK, i=LINE // 4),
             w4_raw[:].rearrange("p (g i t) -> p g t i", t=PACK, i=LINE // 4),
         )
 
         h_banks = [psum.tile([P, PACK, CHUNK], F32, name="h_bank_%d" % c) for c in range(CHUNKS)]
-        order = [["e", "x", "y"]] * (CHUNKS - 1) + [["e", "y", "x"]]
+        order = [["e", "y", "x"]] * (CHUNKS - 1) + [["e", "x", "y"]]
 
         def first_passes(c, name):
             cols = slice(c * CHUNK, (c + 1) * CHUNK)
@@ -184,9 +180,9 @@ def tile_picked_zlayout_silu_po_kernel(
                     stop=(name == order[c][-1] and t == PACK - 1),
                 )
 
-        for name in ("e", "x"):
+        for name in ("e", "y"):
             for c in range(CHUNKS):
-                if name in order[c][: order[c].index("y")]:
+                if name in order[c][: order[c].index("x")]:
                     first_passes(c, name)
 
         out_words = sbuf_tile([P, S], I32, "out_words")
@@ -199,7 +195,7 @@ def tile_picked_zlayout_silu_po_kernel(
 
         def first_product(c):
             h_bf16 = sbuf_tile([P, CHUNK, PACK], BF16, "h_bf16_%d" % c)
-            for name in order[c][order[c].index("y") :]:
+            for name in order[c][order[c].index("x") :]:
                 first_passes(c, name)
             nc.scalar.activation(h_bf16[:], h_banks[c][:].rearrange("p t n -> p n t"), SILU)
             activated[c] = h_bf16

@@ -207,15 +207,16 @@ def tile_picked_zlayout_silu_po_kernel(
             nc.vector.quantize_mx(out=h_codes[:].bitcast(FP8X4), scales=h_scales[:], in_=h_bf16[:].rearrange("p n t -> p (n t)"))
             hidden[c] = (h_codes, h_scales)
 
-        def second_product(c):
-            cols = slice(c * CHUNK, (c + 1) * CHUNK)
+        banks = {}
+
+        def second_passes(c, t0, t1, tag):
             h_codes, h_scales = hidden[c]
-            result[c] = sbuf_tile([P, PACK, CHUNK], F32, "result_%d" % c)
-            bank = psum.tile([P, PACK, CHUNK], F32, name="out_bank_%d" % c)
-            for t in range(PACK):
+            bank = psum.tile([P, t1 - t0, CHUNK], F32, name=tag)
+            banks[c, t0] = bank
+            for t in range(t0, t1):
                 m_cols = slice(t * P, (t + 1) * P)
                 nc.tensor.matmul_mx(
-                    out=bank[:, t, :],
+                    out=bank[:, t - t0, :],
                     lhsT=w4_dealt[:, m_cols].bitcast(FP8X4),
                     lhsT_scale=w4_placed[W4_FIRST:, m_cols],
                     rhs=h_codes[:].bitcast(FP8X4),
@@ -223,9 +224,15 @@ def tile_picked_zlayout_silu_po_kernel(
                     start=True,
                     stop=True,
                 )
-            copy = nc.vector.tensor_copy if c == 0 else nc.scalar.copy
-            copy(result[c][:], bank[:])
-            nc.sync.dma_start(out=out_rows[:, :, cols], in_=result[c][:])
+
+        def empty_bank(c, t0, t1, copy):
+            if t0 == 0:
+                result[c] = sbuf_tile([P, PACK, CHUNK], F32, "result_%d" % c)
+            copy(result[c][:, t0:t1, :], banks[c, t0][:])
+            nc.sync.dma_start(out=out_rows[:, t0:t1, c * CHUNK : (c + 1) * CHUNK], in_=result[c][:, t0:t1, :])
+
+        def round_bank(c):
+            nc.scalar.copy(out_bf16[:, c * CHUNK : (c + 1) * CHUNK, :], banks[c, 0][:].rearrange("p t n -> p n t"))
 
         def round_result(c):
             nc.vector.tensor_copy(
@@ -244,21 +251,27 @@ def tile_picked_zlayout_silu_po_kernel(
         for c in range(CHUNKS):
             first_product(c)
         quantize_hidden(0)
-        for c in range(CHUNKS):
-            if c + 1 < CHUNKS:
-                quantize_hidden(c + 1)
-            second_product(c)
-
-        half = CHUNKS // 2
-        for c in range(half):
-            round_result(c)
-        for c in range(half):
-            quantize_result(c, c + 1)
-        store_words(0, half)
-        for c in range(half, CHUNKS):
-            round_result(c)
-        quantize_result(half, CHUNKS)
-        store_words(half, CHUNKS)
+        quantize_hidden(1)
+        second_passes(0, 0, PAIR, "out_bank_0")
+        second_passes(0, PAIR, PACK, "h_bank_0")
+        empty_bank(0, 0, PAIR, nc.vector.tensor_copy)
+        quantize_hidden(2)
+        empty_bank(0, PAIR, PACK, nc.vector.tensor_copy)
+        second_passes(1, 0, PACK, "out_bank_1")
+        empty_bank(1, 0, PACK, nc.scalar.copy)
+        quantize_hidden(3)
+        for c in range(2, CHUNKS):
+            second_passes(c, 0, PACK, "out_bank_%d" % c)
+            empty_bank(c, 0, PACK, nc.scalar.copy)
+        round_bank(CHUNKS - 1)
+        round_result(0)
+        round_result(1)
+        quantize_result(0, 1)
+        quantize_result(1, 2)
+        round_result(2)
+        quantize_result(2, 3)
+        quantize_result(3, 4)
+        store_words(0, CHUNKS)
 
         for r in range(4):
             queue = nc.sync if r % 2 == 0 else nc.scalar

from contextlib import ExitStack

import concourse.mybir as mybir

K, T, S, W, H, N = 512, 2048, 512, 1024, 512, 512
FLOPS = 2 * (3 * K * H * S + H * N * S)

F32 = mybir.dt.float32
BF16 = mybir.dt.bfloat16
I32 = mybir.dt.int32
U32 = mybir.dt.uint32
U16 = mybir.dt.uint16
U8 = mybir.dt.uint8
FP8X4 = mybir.dt.float8_e4m3fn_x4
SILU = mybir.ActivationFunctionType.Silu

P = 128
PACK = 4
PAIR = 2
CHUNK = 128
CHUNKS = S // CHUNK
GROUP = 16
LINE = 16
ALIGN = 256
ROWS = 16
SPREAD = P // ROWS
TABLES_FIRST = 4
E_FIRST = 8
W4_FIRST = 12

H_CODES_AT = 0


def tile_picked_zlayout_silu_po_kernel(
    tc, x_words, x_scales, e_words, e_scales, y_words, y_scales, w1, w2, w3, w4_words, w4_scales, offs, tok, row,
    out_0, out_1, out_2,
):
    nc = tc.nc
    with ExitStack() as ctx:
        keep = ctx.enter_context(tc.tile_pool(name="keep", bufs=1))
        shared = ctx.enter_context(tc.tile_pool(name="shared", bufs=1))
        psum = ctx.enter_context(tc.psum_pool(name="psum", bufs=1))

        def sbuf_tile(shape, dtype, name, at=None):
            if at is None:
                return keep.tile(shape, dtype, name=name, align_bytes=ALIGN)
            return shared.tile(shape, dtype, name=name, align_bytes=ALIGN, offset=at)

        def words_view(words):
            return words[0].rearrange("p n t -> p (n t)").bitcast(I32)

        words_in = {"e": e_words, "x": x_words, "y": y_words}
        scales_in = {"e": e_scales, "x": x_scales, "y": y_scales, "w4": w4_scales}
        list_in = {"e": tok, "x": offs, "y": row}
        weight_in = {"e": w2, "x": w1, "y": w3}
        columns = {"e": W, "x": T, "y": W, "w4": N}
        tables = ("y", "x")

        plane = {}
        for name in ("e",) + tables + ("w4",):
            plane[name] = sbuf_tile([P, columns[name]], U8, "plane_" + name)
            nc.vector.memset(plane[name][:].bitcast(I32), 0)
        placed = sbuf_tile([P, len(tables), S], U8, "placed")
        nc.vector.memset(placed[:].bitcast(I32), 0)
        w4_placed = sbuf_tile([P, N], U8, "w4_placed")
        nc.vector.memset(w4_placed[:].bitcast(I32), 0)

        raw, lists, table = {}, {}, {}

        def load_scales(name):
            nc.sync.dma_start(out=plane[name][0:P:SPREAD, :].bitcast(I32), in_=scales_in[name][0].bitcast(I32))

        def load_weight(name, at=None):
            raw[name] = sbuf_tile([P, PACK, H], F32, "raw_" + name, at)
            nc.sync.dma_start(out=raw[name][:], in_=weight_in[name].rearrange("(p j) c -> p j c", j=PACK))

        def load_list(name):
            lists[name] = keep.tile([P, S // GROUP], U16, name="list_" + name)
            nc.sync.dma_start(lists[name][:], list_in[name])

        def load_table(name, at=None):
            table[name] = sbuf_tile([P, columns[name]], I32, "table_" + name, at)
            nc.sync.dma_start(out=table[name][:], in_=words_view(words_in[name]))

        def place(target, first, source):
            for r in range(4):
                nc.sync.dma_start(out=target[first + r : P : 32, :].bitcast(I32), in_=source[SPREAD * r : P : 32, :].bitcast(I32))

        load_table("y")
        load_list("e")
        load_list("y")
        for r in range(4):
            nc.sync.dma_start(out=plane["e"][E_FIRST + r : P : 32, :].bitcast(I32), in_=e_scales[0, r:ROWS:4, :].bitcast(I32))
        load_weight("e")
        load_list("x")
        load_scales("y")
        load_scales("x")
        load_weight("y")
        load_scales("w4")
        load_table("e")
        load_weight("x")

        picked = {}

        def gather_words(name, pieces=1, at=None):
            picked[name] = sbuf_tile([P, S], U32, "picked_" + name, at)
            width = S // pieces
            for c0 in range(0, S, width):
                offsets = lists[name][:, c0 // GROUP : (c0 + width) // GROUP]
                nc.vector.tensor_copy(picked[name][:, c0 : c0 + width], table[name][:].bitcast(U32).indirect(offsets))

        picked_scales = {}
        e_picked = sbuf_tile([P, S], U8, "picked_scales_e")
        nc.vector.tensor_copy(e_picked[:], plane["e"][:].indirect(lists["e"][:]))
        picked_scales["e"] = e_picked[E_FIRST:, :]
        gather_words("y")
        spread = sbuf_tile([P, len(tables), S], U8, "spread")
        for i, name in enumerate(tables):
            nc.vector.tensor_copy(spread[:, i, :], plane[name][:].indirect(lists[name][:]))
            picked_scales[name] = placed[TABLES_FIRST:, i, :]
        place(placed[:].rearrange("p i n -> p (i n)"), TABLES_FIRST, spread[:].rearrange("p i n -> p (i n)"))

        load_table("x")
        w4_raw = sbuf_tile([P, N], I32, "w4_raw")
        nc.sync.dma_start(out=w4_raw[:], in_=words_view(w4_words))

        rounded, w_codes, w_scales = {}, {}, {}

        def round_weight(name, copy, t0, t1, at=None):
            rounded[name, t0] = sbuf_tile([P, t1 - t0, P, PACK], BF16, "rounded_%s_%d" % (name, t0), at)
            copy(
                rounded[name, t0][:].rearrange("p t m j -> p m j t"),
                raw[name][:].rearrange("p j (m t) -> p m j t", t=PACK)[:, :, :, t0:t1],
            )

        def quantize_weight(name, t0, t1):
            codes = sbuf_tile([P, (t1 - t0) * P], U32, "w_codes_%s_%d" % (name, t0))
            scales = sbuf_tile([P, (t1 - t0) * P], U8, "w_scales_%s_%d" % (name, t0))
            nc.vector.quantize_mx(out=codes[:].bitcast(FP8X4), scales=scales[:], in_=rounded[name, t0][:].rearrange("p t m j -> p (t m j)"))
            for t in range(t0, t1):
                w_codes[name, t] = codes[:, (t - t0) * P : (t - t0 + 1) * P]
                w_scales[name, t] = scales[:, (t - t0) * P : (t - t0 + 1) * P]

        round_weight("e", nc.scalar.copy, 0, PACK)
        quantize_weight("e", 0, PACK)
        round_weight("y", nc.scalar.copy, 0, PACK)
        w4_spread = sbuf_tile([P, N], U8, "w4_spread")
        nc.vector.tensor_copy(
            w4_spread[:].rearrange("p (t g i) -> p g t i", t=PACK, i=LINE),
            plane["w4"][:].rearrange("p (g i t) -> p g t i", t=PACK, i=LINE),
        )
        place(w4_placed[:], W4_FIRST, w4_spread[:])
        gather_words("e", CHUNKS)
        quantize_weight("y", 0, PACK)
        round_weight("x", nc.scalar.copy, 0, PAIR)
        round_weight("x", nc.vector.tensor_copy, PAIR, PACK)
        quantize_weight("x", PAIR, PACK)
        quantize_weight("x", 0, PAIR)
        gather_words("x", CHUNKS)

        w4_dealt = sbuf_tile([P, N], I32, "w4_dealt")
        nc.vector.tensor_copy(
            w4_dealt[:].rearrange("p (t g i) -> p g t i", t=PACK, i=LINE // 4),
            w4_raw[:].rearrange("p (g i t) -> p g t i", t=PACK, i=LINE // 4),
        )

        h_banks = [psum.tile([P, PACK, CHUNK], F32, name="h_bank_%d" % c) for c in range(CHUNKS)]
        order = [["e", "y", "x"]] * (CHUNKS - 1) + [["e", "x", "y"]]

        def first_passes(c, name):
            cols = slice(c * CHUNK, (c + 1) * CHUNK)
            for t in range(PACK):
                nc.tensor.matmul_mx(
                    out=h_banks[c][:, t, :],
                    lhsT=w_codes[name, t].bitcast(FP8X4),
                    lhsT_scale=w_scales[name, t],
                    rhs=picked[name][:, cols].bitcast(FP8X4),
                    rhs_scale=picked_scales[name][:, cols],
                    start=(name == order[c][0] and t == 0),
                    stop=(name == order[c][-1] and t == PACK - 1),
                )

        for name in ("e", "y"):
            for c in range(CHUNKS):
                if name in order[c][: order[c].index("x")]:
                    first_passes(c, name)

        out_words = sbuf_tile([P, S], I32, "out_words")
        out_scales = sbuf_tile([P, S], U8, "out_scales")
        out_bf16 = sbuf_tile([P, S, PACK], BF16, "out_bf16")
        out_rows = out_0.rearrange("(p t) j -> p t j", t=PACK)
        hidden, result = {}, {}

        activated = {}

        def first_product(c):
            h_bf16 = sbuf_tile([P, CHUNK, PACK], BF16, "h_bf16_%d" % c)
            for name in order[c][order[c].index("x") :]:
                first_passes(c, name)
            nc.scalar.activation(h_bf16[:], h_banks[c][:].rearrange("p t n -> p n t"), SILU)
            activated[c] = h_bf16

        def quantize_hidden(c):
            h_bf16 = activated[c]
            h_codes = sbuf_tile([P, CHUNK], U32, "h_codes_%d" % c, H_CODES_AT + (c % 2) * 4 * CHUNK)
            h_scales = sbuf_tile([P, CHUNK], U8, "h_scales_%d" % c)
            nc.vector.quantize_mx(out=h_codes[:].bitcast(FP8X4), scales=h_scales[:], in_=h_bf16[:].rearrange("p n t -> p (n t)"))
            hidden[c] = (h_codes, h_scales)

        banks = {}

        def second_passes(c, t0, t1, tag):
            h_codes, h_scales = hidden[c]
            bank = psum.tile([P, t1 - t0, CHUNK], F32, name=tag)
            banks[c, t0] = bank
            for t in range(t0, t1):
                m_cols = slice(t * P, (t + 1) * P)
                nc.tensor.matmul_mx(
                    out=bank[:, t - t0, :],
                    lhsT=w4_dealt[:, m_cols].bitcast(FP8X4),
                    lhsT_scale=w4_placed[W4_FIRST:, m_cols],
                    rhs=h_codes[:].bitcast(FP8X4),
                    rhs_scale=h_scales[:],
                    start=True,
                    stop=True,
                )

        def empty_bank(c, t0, t1, copy):
            if t0 == 0:
                result[c] = sbuf_tile([P, PACK, CHUNK], F32, "result_%d" % c)
            copy(result[c][:, t0:t1, :], banks[c, t0][:])
            nc.sync.dma_start(out=out_rows[:, t0:t1, c * CHUNK : (c + 1) * CHUNK], in_=result[c][:, t0:t1, :])

        def round_bank(c):
            nc.scalar.copy(out_bf16[:, c * CHUNK : (c + 1) * CHUNK, :], banks[c, 0][:].rearrange("p t n -> p n t"))

        def round_result(c):
            nc.vector.tensor_copy(
                out_bf16[:, c * CHUNK : (c + 1) * CHUNK, :].rearrange("p (g i) t -> p g t i", i=LINE // 4),
                result[c][:].rearrange("p t (g i) -> p g t i", i=LINE // 4),
            )

        def quantize_result(c0, c1):
            cols = slice(c0 * CHUNK, c1 * CHUNK)
            nc.vector.quantize_mx(out=out_words[:, cols].bitcast(FP8X4), scales=out_scales[:, cols], in_=out_bf16[:, cols, :].rearrange("p n t -> p (n t)"))

        def store_words(c0, c1):
            cols = slice(c0 * CHUNK, c1 * CHUNK)
            nc.sync.dma_start(out=words_view(out_1)[:, cols], in_=out_words[:, cols])

        for c in range(CHUNKS):
            first_product(c)
        quantize_hidden(0)
        quantize_hidden(1)
        second_passes(0, 0, PAIR, "out_bank_0")
        second_passes(0, PAIR, PACK, "h_bank_0")
        empty_bank(0, 0, PAIR, nc.vector.tensor_copy)
        quantize_hidden(2)
        empty_bank(0, PAIR, PACK, nc.vector.tensor_copy)
        second_passes(1, 0, PACK, "out_bank_1")
        empty_bank(1, 0, PACK, nc.scalar.copy)
        quantize_hidden(3)
        for c in range(2, CHUNKS):
            second_passes(c, 0, PACK, "out_bank_%d" % c)
            empty_bank(c, 0, PACK, nc.scalar.copy)
        round_bank(CHUNKS - 1)
        round_result(0)
        round_result(1)
        quantize_result(0, 1)
        quantize_result(1, 2)
        round_result(2)
        quantize_result(2, 3)
        quantize_result(3, 4)
        store_words(0, CHUNKS)

        for r in range(4):
            queue = nc.sync if r % 2 == 0 else nc.scalar
            queue.dma_start(out=out_2[0, r:16:4, :].bitcast(I32), in_=out_scales[r:P:32, :].bitcast(I32))
